import numpy as np, ml_dtypes
CORES = [40,64,80,88,96,104,120,144]
N = 8
BF = ml_dtypes.bfloat16
C, L, S0, K, T, R, Q = 2048, 256, 512, 16, 3, 11, 9
M, S = C // L, S0 + L * T
def perms(rng):
    return np.ascontiguousarray(np.argsort(rng.random((N, 8, S0)), axis=-1))
def parts(rng):
    x = np.floor(rng.random((N, 8, 16, C)) * rng.integers(160, 257, (N, 8, 1, C))).astype(np.int64)
    v = np.floor(rng.random((N, 8, 16, S0)) * rng.integers(96, 257, (N, 8, 1, S0))).astype(np.int64)
    w = rng.integers(0, S0, (N, 8, C)); few = rng.integers(0, S0, (N, 8, 16))
    w = np.where(rng.random((N, 8, C)) < 0.25, np.take_along_axis(few, rng.integers(0, 16, (N, 8, C)), 2), w)
    th = rng.integers(48, 208, (N, 8, 1, T)) + rng.integers(-16, 17, (N, 8, 16, T))
    return x, v, perms(rng), perms(rng), w, th
def pack(x, v, e, h, w, th):
    big = lambda a: np.ascontiguousarray(a.reshape(N, 128, -1)).astype(np.float32).astype(BF)
    return {"x0": big(x), "v0": big(v), "e0": e.astype(np.int32), "h0": h.astype(np.int32), "w0": w.astype(np.int32), "th": big(th)}
def put(p, s, at):
    j = int(np.argmax(p == at)); p[j] = p[s]; p[s] = at
def setup_inputs(rng):
    return pack(*parts(rng))
def setup_inputs_spread(rng):
    x, v, e, h, w, th = parts(rng)
    x = np.floor(np.exp2(8 * rng.random((N, 8, 1, C))) * rng.random((N, 8, 16, C)) * (rng.random((N, 8, 1, C)) > 0.0625)).astype(np.int64)
    v = np.floor(np.exp2(8 * rng.random((N, 8, 1, S0)) * rng.random((N, 8, 1, S0))) * rng.random((N, 8, 16, S0)) * (rng.random((N, 8, 1, S0)) > 0.0625)).astype(np.int64)
    w = np.minimum(np.floor(S0 * rng.random((N, 8, C)) ** 3).astype(np.int64), S0 - 1)
    th = np.floor(np.exp2(8 * rng.random((N, 8, 1, T))) * rng.random((N, 8, 16, T))).astype(np.int64)
    return pack(x, v, e, h, w, th)
def setup_inputs_ends(rng):
    bx = rng.choice(np.array([0.0, 0.1, 0.5, 0.9, 1.0, 1.0]), (N, 8, 1, C)); bv = rng.choice(np.array([0.0, 0.1, 0.5, 0.9, 1.0]), (N, 8, 1, S0))
    bx[:, 7] = rng.choice(np.array([0.0, 0.0, 0.1, 0.1, 1.0]), (N, 1, C)); bx[:, 7, :, ::64] = 0.0
    x = 255 * (rng.random((N, 8, 16, C)) < bx).astype(np.int64); v = 255 * (rng.random((N, 8, 16, S0)) < bv).astype(np.int64)
    w = np.where(rng.random((N, 8, C)) < 0.75, (S0 - 1) * rng.integers(0, 2, (N, 8, C)), rng.integers(0, S0, (N, 8, C)))
    e, h = perms(rng), perms(rng)
    th = 255 * (rng.random((N, 8, 16, T)) < rng.choice(np.array([0.0, 0.25, 0.5, 0.75, 1.0]), (N, 8, 1, T))).astype(np.int64); th[:, 0, :, 0] = 0; th[:, 5, :, T - 1] = 255
    v[..., 0] = 255 * rng.integers(0, 2, (N, 8, 1)); v[..., S0 - 1] = 255 * rng.integers(0, 2, (N, 8, 1))
    v[:, 7, :, 0] = 255; v[:, 7, :, S0 - 1] = 255; w[:, 7] = np.where(((np.arange(C) >> 9) & 1) == 1, 0, S0 - 1)
    v[:, 0, :, 1] = 0; v[:, 0, 15, 1] = 132; v[:, 0, 1, 1] = 1
    v[:, 7, :, L - 2] = 255; v[:, 7, 15, L - 2] = 132; v[:, 7, 13, L - 2] = 254; v[:, 7, 0, L - 2] = 254
    for r in range(N):
        for g in range(8):
            opp = g == 7 or (g & 1) == 0
            put(e[r, g], 0, 0); put(e[r, g], S0 - 1, S0 - 1)
            put(h[r, g], 0, S0 - 1 if opp else 0); put(h[r, g], S0 - 1, 0 if opp else S0 - 1)
        if r & 1: x[r, 6] = 255; v[r, 6] = 0; th[r, 6] = 0
    return pack(x, v, e, h, w, th)
def setup_inputs_corners(rng):
    x, v, e, h, w, th = parts(rng); shift = int(rng.integers(0, 8))
    for r in range(N):
        for g in range(8):
            m = (r + g + shift) & 7; two = rng.permutation(L)[:2]; s1, s2 = int(two[0]), int(two[1])
            if m == 0:
                x[r, g] = 0; v[r, g][:, two] = 255; v[r, g][8, two] = 254; w[r, g] = np.where(((np.arange(C) >> 9) & 1) == 1, s1, s2)
                put(e[r, g], s1, 0); put(e[r, g], s2, 1); put(h[r, g], s1, S0 - 1); put(h[r, g], s2, S0 - 2)
            elif m == 1:
                x[r, g] = rng.integers(0, 100, (16, C)); v[r, g][:, s1] = rng.integers(100, 256, 16); w[r, g] = s1
                put(e[r, g], s1, 0); put(h[r, g], s1, S0 - 1)
            elif m == 2: x[r, g] = 255; v[r, g] = 0; th[r, g] = 0
            elif m == 3: x[r, g] = 255; v[r, g] = 0; v[r, g][:, s1] = 255; th[r, g] = 1
            elif m == 4: w[r, g] = rng.choice(np.array([0, S0 - 1, s1, s2]), C)
            elif m == 5: h[r, g] = e[r, g]
            elif m == 6: h[r, g] = S0 - 1 - e[r, g]
            else: th[r, g] = 255; x[r, g] = np.minimum(x[r, g], 254)
    return pack(x, v, e, h, w, th)
def setup_inputs_crowd(rng):
    x, v, e, h, w, th = parts(rng); o = int(rng.integers(0, N)); other = (o + 1 + int(rng.integers(0, N - 1))) & (N - 1); B = 16 * N
    c = rng.integers(96, 256, (N, 8, 16, 1)); c[:, :, 0] = 255
    d = np.zeros((N, 8, L), np.int64) + ((o - np.arange(N)) & (N - 1))[:, None, None]
    for g, i in ((1, int(rng.integers(0, L))), (5, L - 1)): d[other, g, i] = (d[other, g, i] + 1) & (N - 1)
    z = np.floor(rng.random((N, 8, 16, S0)) * (c + 1)).astype(np.int64)
    z0 = 16 * d + rng.integers(0, 16, (N, 8, L)) - np.sum(z[:, :, 1:, :L] * (2 * np.arange(1, 16) + 1)[:, None], axis=2)
    z[:, :, 0, :L] = (z0 & (B - 1)) + B * rng.integers(0, 256 // B, (N, 8, L))
    return pack(np.zeros_like(x) + c, c - z, e, h, w, th)
def setup_inputs_ties(rng):
    e, h, w = perms(rng), perms(rng), rng.integers(0, S0, (N, 8, C)); one = rng.random((N, 8, 1, 1)) < 0.5; one[:, 0] = True; one[:, 7] = False
    st = np.where(one, 1, 32); v = np.where(one, rng.integers(1, 255, (N, 8, 16, S0)), 32 * rng.integers(1, 7, (N, 8, 16, S0)))
    n = rng.choice(np.array([R - 1] * 12 + [R, 0, 16, R - 1]), (N, 8, 1, C)); less = np.argsort(rng.random((N, 8, 16, C)), axis=2) < n
    x = np.take_along_axis(v, w[:, :, None, :], 3) + st * np.where(less, -1, np.where(rng.random((N, 8, 16, C)) < 0.25, 1, 0))
    th = np.where(one, rng.integers(32, 200, (N, 8, 16, T)), 32 * rng.integers(1, 7, (N, 8, 16, T)))
    return pack(x, v, e, h, w, th)
def check_inputs(d):
    bad = []
    for k, lo, hi in (("x0", 0, 255), ("v0", 0, 255), ("e0", 0, S0 - 1), ("h0", 0, S0 - 1), ("w0", 0, S0 - 1), ("th", 0, 255)):
        a = np.asarray(d[k]).astype(np.float64)
        if not np.all((a >= lo) & (a <= hi) & (a == np.floor(a))): bad.append("range of " + k)
    for k in ("e0", "h0"):
        if not np.all(np.sort(np.asarray(d[k]), axis=-1) == np.arange(S0)): bad.append("permutation " + k)
    return bad
def mark(z):
    return np.sum(z.astype(np.int64) * (2 * np.arange(16) + 1)[:, None], axis=2) & 4095
def reference(x0, v0, e0, h0, w0, th):
    take = np.take_along_axis
    X = x0.astype(np.float32).astype(np.int32).reshape(N, 8, 16, C); W = w0.astype(np.int64)
    V = np.zeros((N, 8, 16, S), np.int32); V[..., :S0] = v0.astype(np.float32).astype(np.int32).reshape(N, 8, 16, S0)
    E = np.full((N, 8, S), -1, np.int64); E[..., :S0] = e0; H = np.full((N, 8, S), -1, np.int64); H[..., :S0] = h0
    thr = th.astype(np.float32).astype(np.int32).reshape(N, 8, 16, T)
    lane = np.arange(L); k = np.arange(K); kap = k * k + k + 1; lower = lane[None, :] < lane[:, None]
    y = V[..., :L] + 0; cur = np.zeros((N, 8, L), np.int64) + lane; A = np.zeros((N, 8), np.int64)
    for t in range(T):
        u = mark(y)
        a = (((u * u) >> 5)[..., None] + kap * u[..., None] + A[:, :, None, None]) & (C - 1)
        a = a.reshape(N, 8, L * K); s = take(W, a, 2)
        xa = take(X, a[:, :, None, :], 3).reshape(N, 8, 16, L, K); vs = take(V, s[:, :, None, :], 3).reshape(N, 8, 16, L, K)
        es = take(E, s, 2).reshape(N, 8, L, K); hs = take(H, s, 2).reshape(N, 8, L, K)
        par = (es < take(E, cur, 2)[..., None]) != (hs < take(H, cur, 2)[..., None])
        hit = par & (np.sum(vs > xa, axis=2) >= R)
        race = np.any(hit, axis=3); f = np.argmax(hit, axis=3)
        ff = f[:, :, None, :, None]; vf = take(vs, ff, 4)[..., 0]; xf = take(xa, ff, 4)[..., 0]
        yn = np.where(race[:, :, None, :], np.abs(vf - xf), np.abs(np.max(xa, axis=4) - y))
        new = np.where(race, take(s.reshape(N, 8, L, K), f[..., None], 3)[..., 0], cur)
        lead = ~race & ~np.any((cur[..., :, None] == cur[..., None, :]) & ~race[..., None, :] & lower, axis=3)
        will = np.sum(yn >= thr[..., t:t + 1], axis=2) >= Q
        for r in range(N):
            for g in range(8):
                i = np.flatnonzero(lead[r, g] & ~will[r, g]); V[r, g][:, cur[r, g, i]] = yn[r, g][:, i]
                i = np.flatnonzero(lead[r, g] & will[r, g]); c = cur[r, g, i]; n = S0 + L * t + i
                V[r, g][:, n] = yn[r, g][:, i]; new[r, g, i] = n
                fe = np.zeros(S, np.int64); fe[E[r, g, c]] = 1; fh = np.zeros(S, np.int64); fh[H[r, g, c]] = 1
                old = np.flatnonzero(E[r, g] >= 0); pe = E[r, g, old]; ph = H[r, g, old]
                E[r, g, old] = pe + (np.add.accumulate(fe) - fe)[pe]; H[r, g, old] = ph + np.add.accumulate(fh)[ph]
                E[r, g, n] = E[r, g, c] + 1; H[r, g, n] = H[r, g, c] - 1
        q = (np.arange(N)[:, None, None] + ((mark(yn) >> 4) & (N - 1))) & (N - 1)
        ya = np.ascontiguousarray(yn[q, np.arange(8)[None, :, None], :, lane[None, None, :]].transpose(0, 1, 3, 2))
        b = M * lane + (mark(ya) & (M - 1))
        np.put_along_axis(X, b[:, :, None, :], ya, 3); np.put_along_axis(W, b, new, 2)
        A = np.sum(race, axis=2); y, cur = yn, new
    return {"yx": X.reshape(N, 128, C).astype(np.float32).astype(BF), "yv": V.reshape(N, 128, S).astype(np.float32).astype(BF), "yw": W.astype(np.float32), "ye": E.astype(np.float32), "yh": H.astype(np.float32)}

@@ -1,0 +1,755 @@
+from concourse.bass import DstId, RemoteDMATransfer
+from concourse.mybir import AluOpType, ActivationFunctionType
+
+AL = AluOpType
+AF = ActivationFunctionType
+NR = 3
+NDV = 2
+T_CYCLE, T_CALL, T_WAKE, T_LOOK, T_PE, T_DMA, T_EXCH = 0.001, 0.05, 0.06, 0.5, 0.0005, 2.0, 9.5
+T_GATHER, T_SCATTER = 1.56, 3.8
+PASSES, SHAKE, SEED = 600, 0.5, 4
+NA = [0, 2, 2]
+NTAIL = 0
+ORDER = {}
+
+SCRATCH = {
+    "XE": ("sbuf", [128, 2304], "bfloat16"),
+    "VE": ("sbuf", [128, 1792], "bfloat16"),
+    "PT": ("sbuf", [128, 2304], "bfloat16"),
+    "SP": ("sbuf", [128, 1280], "bfloat16"),
+    "G": ("sbuf", [128, 4096], "bfloat16"),
+    "GT": ("sbuf", [128, 2048], "bfloat16"),
+    "VW": ("sbuf", [128, 2048], "bfloat16"),
+    "EQ": ("sbuf", [128, 4096], "bfloat16"),
+    "land0": ("sbuf", [128, 2048], "bfloat16"),
+    "land1": ("sbuf", [128, 2048], "bfloat16"),
+    "land2": ("sbuf", [128, 2048], "bfloat16"),
+    "B": ("sbuf", [128, 7680], "bfloat16"),
+    "F": ("sbuf", [128, 5440], "float32"),
+    "J": ("sbuf", [128, 2448], "int32"),
+    "M": ("sbuf", [128, 2592], "bfloat16"),
+    "sf": ("sbuf", [128, 1024], "float32"),
+    "si": ("sbuf", [128, 320], "int32"),
+    "su": ("sbuf", [128, 1152], "uint16"),
+    "cf": ("sbuf", [128, 112], "float32"),
+    "thb": ("sbuf", [128, 8], "bfloat16"),
+    "EH": ("sbuf", [128, 512], "int32"),
+    "EA": ("sbuf", [128, 1024], "bfloat16"),
+    "IH": ("sbuf", [128, 1024], "bfloat16"),
+    "S2": ("sbuf", [128, 1792], "bfloat16"),
+    "S1": ("sbuf", [128, 1552], "bfloat16"),
+    "S0": ("sbuf", [128, 512], "bfloat16"),
+    "SE": ("sbuf", [128, 1024], "bfloat16"),
+    "MK": ("sbuf", [128, 1024], "bfloat16"),
+    "CE": ("sbuf", [128, 1040], "float32"),
+    "RA": ("sbuf", [128, 512], "float32"),
+    "RR": ("sbuf", [128, 2048], "float32"),
+}
+for _i in range(8):
+    SCRATCH["p%d" % _i] = ("psum", [128, 512], "float32")
+
+SEMAPHORES = ["cv", "ca", "ct", "cg", "sent"] + ["arr%d" % _i for _i in range(NR)] + ["d%d" % _i for _i in range(20)]
+
+
+def routes(T, topo):
+    cores = list(T.cores)
+    n = len(cores)
+    out = []
+    for r, c in enumerate(cores):
+        order = [(r + d) % n for d in range(1, n)]
+        near = [q for q in order if topo.may_write(c, cores[q])]
+        far = [q for q in order if q not in near]
+        able = [h for h in topo.cores_of(c) if h != c and T.rank_of(h) is None and all(topo.may_write(h, cores[q]) for q in order)]
+        turn = far + near
+        out.append([(h, turn[i::len(able)]) for i, h in enumerate(able)])
+    return out
+
+
+def bits(engs):
+    m = 0
+    for e in engs:
+        m |= 1 << e
+    return m
+
+
+def rank_program(g, core, T, topo):
+    rank = T.rank_of(core)
+    cores = list(T.cores)
+    n = len(cores)
+    rt = routes(T, topo)
+    sem = T.sem
+
+    def slot(t, src, dst):
+        d = (src - dst) % n
+        return T["land%d" % t][:, 256 * d:256 * d + 256]
+
+    def first_hop(r):
+        c = cores[r]
+        on = topo.engines(c, rt[r][0][0])
+        k = len(on) // len(rt[r])
+        return [(h, 0, on[i * k:(i + 1) * k]) for i, (h, _) in enumerate(rt[r])]
+
+    if rank is None:
+        for r in range(n):
+            for (h, qs) in rt[r]:
+                if h != core:
+                    continue
+                got = [len(e) for (d, _, e) in first_hop(r) if d == core][0]
+                engs = topo.engines(core, cores[qs[0]])
+                for t in range(NR):
+                    g.wait_ge(sem["arr%d" % t], got)
+                    ids = []
+                    for q in qs:
+                        rid, pid = topo.addr(cores[q], core)
+                        ids.append(DstId(rid=rid, pnc=pid))
+                    tr = RemoteDMATransfer(dst_ids=ids, dma_engine_mask=bits(engs), remote_sem=sem["arr%d" % t],
+                                           src=T["land%d" % t][:, 0:256], dsts=[slot(t, r, q) for q in qs])
+                    g.remote_dma_fused([tr], local_sem=sem["sent"])
+                g.wait_ge(sem["sent"], NR * len(engs))
+        return
+
+    arrivals = 0
+    for r in range(n):
+        for (h, qs) in rt[r]:
+            if rank in qs:
+                arrivals += len(topo.engines(h, cores[qs[0]]))
+
+    Q = {"v": g.vector, "a": g.scalar, "t": g.tensor, "g": g, "s": g.sync}
+    SN = {"v": "cv", "a": "ca", "t": "ct", "g": "cg"}
+    cnt = {}
+    known = {e: {} for e in Q}
+    recs = {}
+    ndma = [0]
+    nodes = []
+
+    def R(name, a=None, b=None, s=1, p=None):
+        t = T[name]
+        if a is None:
+            a, b = 0, t.shape[1]
+        ps = slice(0, 128) if p is None else slice(*p)
+        two = SCRATCH[name][2] in ("bfloat16", "uint16")
+        return (t[ps, a:b:s] if s != 1 else t[ps, a:b], [(name, a, b)], [], len(range(a, b, s)), two)
+
+    def IX(win, off):
+        return (win[0].indirect(off[0]), win[1], off[1], 16 * off[3], win[4])
+
+    def need(e, tok):
+        if known[e].get(tok[0], 0) < tok[1]:
+            Q[e].wait_ge(sem[tok[0]], tok[1])
+            known[e][tok[0]] = tok[1]
+
+    def emit(e, fn, outs, ins, kind="c", rate=1.0, time=None, late=0.0):
+        wr, rd = [], []
+        full = [x for x in ins if isinstance(x, tuple)]
+        for o in outs:
+            wr += o[1]
+            rd += o[2]
+        for i in full:
+            rd += i[1] + i[2]
+        if time is None:
+            o = outs[0]
+            if o[2]:
+                cyc = T_SCATTER * o[3]
+            elif any(i[2] for i in full):
+                cyc = T_GATHER * o[3]
+            else:
+                if rate == 0.5 and not (o[4] and all(i[4] for i in full if i[3] > 1)):
+                    rate = 1.0
+                cyc = max(64.0, rate * max([o[3]] + [i[3] for i in full]))
+            time = T_CALL + cyc * T_CYCLE
+        who = e if kind == "c" else "x%d" % len(nodes)
+        deps = set()
+        for w, regs in ((True, wr), (False, rd)):
+            for (nm, a, b) in regs:
+                ps = SCRATCH[nm][0] == "psum"
+                for (a2, b2, nd, w2, e2) in recs.get(nm, []):
+                    if (ps and (e2 != e or e == "t")) or (a < b2 and a2 < b and (w or w2)):
+                        deps.add(nd)
+        me = len(nodes)
+        nodes.append({"e": e, "fn": fn, "kind": kind, "time": time, "late": late, "deps": deps})
+        for (nm, a, b) in wr:
+            ps = SCRATCH[nm][0] == "psum"
+            recs[nm] = [x for x in recs.get(nm, []) if not (a <= x[0] and x[1] <= b) and not (ps and e == "t")]
+            recs[nm].append((a, b, me, True, who))
+        for (nm, a, b) in rd:
+            recs.setdefault(nm, []).append((a, b, me, False, who))
+        return me
+
+    def issue():
+        m = len(nodes)
+        kids = [[] for _ in range(m)]
+        for i, nd in enumerate(nodes):
+            for d in nd["deps"]:
+                kids[d].append(i)
+        rest = [0.0] * m
+        for i in range(m - 1, -1, -1):
+            rest[i] = nodes[i]["time"] + nodes[i]["late"] + max([rest[k] + T_WAKE for k in kids[i]] + [0.0])
+        pars = [sorted(nd["deps"]) for nd in nodes]
+        eng = [nd["e"] for nd in nodes]
+
+        def plan(before, after, prio, back):
+            left = [len(x) for x in before]
+            at = [nodes[i]["late"] if back else 0.0 for i in range(m)]
+            ready = {e: [i for i in range(m) if left[i] == 0 and eng[i] == e] for e in Q}
+            free = {e: 0.0 for e in Q}
+            end = [0.0] * m
+            seq = []
+            for _ in range(m):
+                t1, e = min((min(max(at[i], free[e]) + nodes[i]["time"] for i in ready[e]), e) for e in Q if ready[e])
+                t0 = max(min(at[i] for i in ready[e]), free[e])
+                i = max([j for j in ready[e] if at[j] <= t0 + T_LOOK * (t1 - t0)], key=lambda j: (prio[j], -j))
+                ready[e].remove(i)
+                seq.append(i)
+                free[e] = max(at[i], free[e]) + nodes[i]["time"]
+                end[i] = free[e] + (0.0 if back else nodes[i]["late"])
+                for k in after[i]:
+                    at[k] = max(at[k], end[i] + T_WAKE + (nodes[k]["late"] if back else 0.0))
+                    left[k] -= 1
+                    if left[k] == 0:
+                        ready[eng[k]].append(k)
+            return max(end), end, seq
+
+        if m not in ORDER:
+            best = None
+            prio = rest
+            x = SEED
+            for _ in range(PASSES):
+                span, end, seq = plan(pars, kids, prio, False)
+                if best is None or span < best[0]:
+                    best = (span, seq, end)
+                end = list(best[2] if span > best[0] + 1.0 else end)
+                for i in range(m):
+                    x = (x * 1103515245 + 12345) % 2147483648
+                    end[i] += SHAKE * x / 2147483648
+                prio = plan(kids, pars, end, True)[1]
+            ORDER[m] = best
+        tok = [None] * m
+        for i in ORDER[m][1]:
+            nd = nodes[i]
+            e = nd["e"]
+            toks = {}
+            for d in nd["deps"]:
+                if not (e == "t" and nodes[d]["e"] == "t"):
+                    toks[tok[d][0]] = max(toks.get(tok[d][0], 0), tok[d][1])
+            for k in sorted(toks):
+                need(e, (k, toks[k]))
+            ins_ = nd["fn"]()
+            if nd["kind"] == "dma":
+                s_ = "d%d" % ndma[0]
+                ndma[0] += 1
+                ins_.then_inc(sem[s_], 16)
+                cnt[s_] = 16
+            elif nd["kind"] == "c":
+                s_ = SN[e]
+                ins_.then_inc(sem[s_], 1)
+                cnt[s_] = cnt.get(s_, 0) + 1
+            else:
+                s_ = nd["kind"]
+                cnt[s_] = arrivals
+            tok[i] = (s_, cnt[s_])
+        for k in sorted(cnt):
+            need("g", (k, cnt[k]))
+
+    def A_(x):
+        return x[0] if isinstance(x, tuple) else x
+
+    def cp(out, in_):
+        emit("v", lambda: g.vector.tensor_copy(out[0], in_[0]), [out], [in_], rate=0.5)
+
+    def tt(out, a, b, op):
+        ps = any(SCRATCH[x[1][0][0]][0] == "psum" for x in (a, b))
+        emit("v", lambda: g.vector.tensor_tensor(out[0], a[0], b[0], op), [out], [a, b], rate=1.0 if ps else 2.0)
+
+    def ts(out, a, s1, op0, s2=None, op1=None):
+        if op1 is None:
+            emit("v", lambda: g.vector.tensor_scalar(out[0], a[0], A_(s1), None, op0), [out], [a, s1], rate=0.5)
+        else:
+            emit("v", lambda: g.vector.tensor_scalar(out[0], a[0], A_(s1), A_(s2), op0, op1), [out], [a, s1, s2], rate=0.5)
+
+    def scan(out, d0, d1, init, op0, op1):
+        emit("v", lambda: g.vector.tensor_tensor_scan(out[0], d0[0], d1[0], init, op0, op1), [out], [d0, d1], rate=0.5)
+
+    def act(out, in_, f, bias=0.0, scale=1.0, acc=None):
+        if acc is None:
+            emit("a", lambda: g.scalar.activation(out[0], in_[0], f, bias=A_(bias), scale=A_(scale)), [out], [in_, bias, scale])
+        else:
+            emit("a", lambda: g.scalar.activation(out[0], in_[0], f, bias=A_(bias), scale=A_(scale), accum_out=acc[0]), [out, acc], [in_, bias, scale])
+
+    def aff(out, in_, scale=1.0, bias=0.0):
+        act(out, in_, AF.Identity, bias=bias, scale=scale)
+
+    def onehot(out, tmp, in_, neg):
+        act(tmp, in_, AF.Abs, bias=neg)
+        act(out, tmp, AF.Relu, bias=1.0, scale=-1.0)
+
+    def mm(items, first=True, last=True):
+        def fn():
+            r_ = None
+            for i, (o, l, r) in enumerate(items):
+                r_ = g.tensor.matmul(o[0], l[0], r[0], first and i == 0, last and i == len(items) - 1)
+            return r_
+        emit("t", fn, [x[0] for x in items], [x[1] for x in items] + [x[2] for x in items],
+             time=sum(max(64, x[2][3]) for x in items) * T_PE)
+
+    def iota(out, pat, base=0, cm=0):
+        emit("g", lambda: g.iota(out[0], pat, base, cm, allow_small_or_imprecise_dtypes=True), [out], [],
+             time=0.13 + 2 * out[3] * T_CYCLE)
+
+    def fill(out, c):
+        iota(out, [[0, out[3]]], c)
+
+    def load(e, out, src):
+        emit(e, lambda: Q[e].dma_start(out[0], src), [out], [], kind="dma", time=0.1, late=T_DMA + out[3] * 0.001)
+
+    def store(e, dst, in_):
+        emit(e, lambda: Q[e].dma_start(dst, in_[0]), [], [in_], kind="dma", time=0.1, late=T_DMA + in_[3] * 0.001)
+
+    def slots(buf, w):
+        names = {}
+
+        def f(name, a=0, b=None, s=1, k=1, p=None):
+            if name not in names:
+                names[name] = (sum(x[1] for x in names.values()), k)
+            o, kk = names[name]
+            return R(buf, o * w + a, o * w + (kk * w if b is None else b), s, p)
+        return f
+
+    Bt, Ft, Jt, Mt = slots("B", 256), slots("F", 272), slots("J", 272), slots("M", 144)
+    sf, si, su, cf = slots("sf", 16), slots("si", 16), slots("su", 16), slots("cf", 1)
+
+    def P(i, a, b):
+        return R("p%d" % i, a, b)
+
+    def to_list(out, z, src):
+        nm, a, b = src[1][0]
+        mm([(out, Mt(z, 15 - y, 143 - y), R(nm, a + y, b, 16)) for y in range(16)])
+
+    def col(name, i):
+        return cf(name, i, i + 1)
+
+    def sq(name):
+        return Mt(name, 0, 128)
+
+    LP = R("PT", 2048, 2304)
+
+    load("a", R("EH", p=(0, 8)), T.e0[:])
+    load("a", (T.EH[8:16, :], [("EH", 600, 601)], [], 512, False), T.h0[:])
+    load("s", Jt("wn", 0, 128), T.w0[:])
+    load("s", R("XE", 2048, 2304), T.v0[:, 0:256])
+    load("s", R("VE", 0, 512), T.v0[:])
+    load("s", R("XE", 0, 2048), T.x0[:])
+    load("s", R("thb", 0, 3), T.th[:])
+    EHall = (T.EH[0:16, :], [("EH", 0, 601)], [], 512, False)
+
+    iota(si("p", 0, 1), [[0, 1]], 0, 1)
+    iota(sf("c1"), [[1, 16]])
+    iota(Ft("n", 0, 144), [[1, 144]])
+    iota(sf("l1"), [[16, 8], [0, 2]])
+    iota(Ft("y", 0, 256), [[0, 16], [1, 16]])
+    iota(R("IH", 0, 512, p=(0, 1)), [[8, 64], [0, 8]])
+    iota(R("IH", 512, 1024, p=(0, 1)), [[0, 64], [1, 8]])
+    iota(Ft("k", 0, 256), [[1, 16], [0, 16]])
+    iota(sf("c16"), [[16, 16]])
+    iota(Ft("j17", 0, 17), [[16, 17]])
+    iota(Ft("pr"), [[-4096, 272]], 272 * 4096)
+    fill(Jt("v", 256, 272), 2048)
+    fill(R("VE", 512, 1792), 0)
+    fill(R("S2"), 1)
+    fill(R("S1", 0, 1536), 1)
+    fill(R("S1", 1536, 1552), 0)
+    fill(Bt("two"), 2)
+    fill(R("CE", 0, 8), 0)
+    fill(sf("D4", 48, 64, k=4), 256)
+
+    ts(si("p", 1, 2), si("p", 0, 1), 15, AL.bitwise_and)
+    ts(si("p", 2, 3), si("p", 0, 1), 4, AL.arith_shift_right)
+    ts(si("p", 3, 4), si("p", 0, 1), 7, AL.bitwise_and)
+    ts(si("p", 4, 5), si("p", 0, 1), 4, AL.arith_shift_right, 1, AL.bitwise_and)
+    ts(si("p", 5, 6), si("p", 0, 1), 3, AL.arith_shift_right, 1, AL.bitwise_and)
+    ts(si("p", 6, 7), si("p", 0, 1), 1, AL.arith_shift_right, 7, AL.bitwise_and)
+    cp(cf("b", 0, 7, k=8), si("p", 0, 7))
+    pf, pm, gi, p7, g0, h8, pq = [col("b", i) for i in range(7)]
+    ts(cf("t2"), p7, 16.0, AL.mult, 1.0, AL.add)
+    ts(cf("t0"), g0, 16.0, AL.mult, h8, AL.add)
+    ts(cf("t3"), h8, 2.0, AL.mult, cf("t2"), AL.add)
+    ts(cf("t1"), p7, 32.0, AL.mult, cf("t0"), AL.add)
+    ts(su("L1"), sf("l1"), pm, AL.add)
+    ts(Mt("selA"), Ft("n", 0, 144), cf("t3"), AL.is_equal)
+    ts(su("L2", 0, 8), sf("c1", 0, 8), 2.0, AL.mult, cf("t1"), AL.add)
+    ts(cf("wm"), pm, 2.0, AL.mult, 1.0, AL.add)
+    ts(cf("zt"), gi, 16.0, AL.mult, 15.0, AL.add)
+    ts(su("Lb"), sf("c1"), 0.0, AL.mult, pm, AL.add)
+    ts(Mt("mark"), Ft("n", 0, 144), cf("zt"), AL.is_equal, cf("wm"), AL.mult)
+
+    aff(cf("nb", 0, 7, k=8), cf("b", 0, 7), -1.0)
+    onehot(cf("oh", k=16), sf("tmp"), sf("c1"), col("nb", 1))
+    aff(cf("t4"), col("oh", 3), 4.0, col("oh", 8))
+    aff(cf("bias0"), col("oh", 1), 4.0, cf("t4"))
+    onehot(Mt("eye"), Ft("tmp", 0, 144), Ft("n", 0, 144), col("nb", 0))
+    aff(cf("pass"), col("oh", 6), -1.0, 1.0)
+    aff(cf("rs"), col("oh", 6), -2.0, 1.0)
+    aff(cf("rb"), col("oh", 6), 11.0)
+    act(Mt("sel"), Ft("y", 0, 144), AF.Relu, bias=-14.0)
+    aff(Mt("dg"), Mt("eye"), cf("pass"))
+    onehot(cf("q", k=8), sf("tmp", 0, 8), sf("c1", 0, 8), col("nb", 6))
+    act(Mt("one"), Mt("mark"), AF.Sign)
+    aff(cf("t5"), col("q", 3), -16777216.0)
+    aff(cf("t6"), col("q", 1), 4.0, cf("t5"))
+    aff(cf("wk"), col("q", 0), 16384.0, cf("t6"))
+    aff(Mt("key"), Mt("one"), cf("wk"))
+    aff(Mt("id"), Mt("one"), col("q", 2))
+    aff(Mt("neye"), Mt("eye"), -1.0)
+    act(Ft("k2", 0, 256), Ft("k", 0, 256), AF.Square, bias=0.5)
+    aff(Ft("kap", 0, 256), Ft("k2", 0, 256), 1.0, 0.75)
+    aff(sf("lane"), sf("c16"), 1.0, pm)
+
+    def tile(t):
+        cp(si("m"), P(2, 0, 16))
+        ts(si("u"), si("m"), 4095, AL.bitwise_and)
+        cp(sf("uf"), si("u"))
+        tt(si("sq"), sf("uf"), sf("uf"), AL.mult)
+        tt(Ft("t1", 0, 256), IX(sf("uf"), su("Lb")), Ft("kap", 0, 256), AL.mult)
+        ts(si("sh"), si("sq"), 5, AL.arith_shift_right)
+        ts(sf("base"), si("sh"), cf("A") if t > 0 else 0.0, AL.add)
+        tt(Jt("s", 0, 256), IX(sf("base"), su("Lb")), Ft("t1", 0, 256), AL.add)
+        ts(Jt("a", 0, 256), Jt("s", 0, 256), 2047, AL.bitwise_and)
+        cp(su("tile", k=16), Jt("a", 0, 256))
+
+    def codes():
+        tt(Ft("code"), IX(Jt("a"), su("Lp", 0, 17, k=2)), Ft("pr"), AL.add)
+
+    def ids(o, w):
+        return [(o, Mt("sel", 11, 139, p=(0, 1)), R("IH", 0, w, p=(0, 1))),
+                (o, Mt("sel", 10, 138, p=(0, 1)), R("IH", 512, 512 + w, p=(0, 1)))]
+
+    cp(R("EA", 0, 512, p=(0, 16)), EHall)
+    tt(R("EA", 512, 1024, p=(0, 16)), EHall, R("EA", 0, 512, p=(0, 16)), AL.subtract)
+    to_list(P(2, 0, 16), "mark", R("XE", 2048, 2304))
+    mm([(P(4, 0, 512), Mt("selA", 1, 129, p=(0, 16)), R("EA", 0, 512, p=(0, 16))),
+        (P(4, 0, 512), Mt("selA", 0, 128, p=(0, 16)), R("EA", 512, 1024, p=(0, 16)))] + ids(P(4, 0, 512), 512))
+    act(R("SP", 0, 512), P(4, 0, 512), AF.Identity, bias=cf("bias0"))
+    cp(Ft("w2", 0, 256), IX(Jt("wn", 0, 128), su("L1")))
+    emit("v", lambda: g.vector.transpose(Ft("w3", 0, 256)[0], Ft("w2", 0, 256)[0]), [Ft("w3", 0, 256)], [Ft("w2", 0, 256)])
+    cp(su("Wl", k=8), IX(Ft("w3", 0, 256), su("L2", 0, 8)))
+    for c in range(2):
+        act(R("PT", 1024 * c, 1024 * c + 1024), IX(R("SP", 0, 512), su("Wl", 64 * c, 64 * c + 64)), AF.Copy)
+    act(LP, R("SP", 0, 256), AF.Copy)
+
+    def blk(c):
+        return 512 * c, 512 * c + 512, su("Wl", 32 * c, 32 * c + 32)
+
+    def greater_v(c, nv):
+        a, b, l = blk(c)
+        tt(R("GT", a, b), IX(R("VE", 0, nv), l), R("XE", a, b), AL.is_gt)
+
+    def fetch_a(c, nv):
+        a, b, l = blk(c)
+        act(R("VW", a, b), IX(R("VE", 0, nv), l), AF.Copy)
+        mm([(P(6 + c % 2, 0, 512), sq("eye"), R("VW", a, b)), (P(6 + c % 2, 0, 512), sq("neye"), R("XE", a, b))])
+
+    def greater_a(c):
+        a, b, l = blk(c)
+        act(R("GT", a, b), P(6 + c % 2, 0, 512), AF.Sign, bias=-0.5)
+
+    def count(c, signs):
+        a, b, l = blk(c)
+        mm([(P(4 + c % 2, 0, 512), sq("dg"), R("PT", a, b)), (P(4 + c % 2, 0, 512), Mt("one", 9, 137), R("GT", a, b))])
+        act(R("PT", a, b), P(4 + c % 2, 0, 512), AF.Relu, bias=cf("rb2" if signs else "rb"), scale=cf("rs2" if signs else "rs"))
+
+    def lane_keys():
+        to_list(P(3, 0, 16), "key", LP)
+        aff(sf("cd"), P(3, 0, 16), 1.0, -float(4096 * 2048 + 2048))
+        act(Ft("cb", 0, 256), IX(sf("cd"), su("Lb")), AF.Copy)
+
+    for c in range(4):
+        greater_v(c, 512)
+        count(c, False)
+    tile(0)
+    lane_keys()
+
+    def cur(t):
+        return sf("cur", 16 * t, 16 * t + 16, k=3)
+
+    def sp(t):
+        return sf("sp", 16 * t, 16 * t + 16, k=4)
+
+    def pre(t):
+        tt(sf("cdm"), cur(t), sf("dum"), AL.subtract)
+        aff(sf("cm"), sf("cdm"), -1.0, 256.0)
+        aff(sf("dn"), sf("cdm"), -1.0, float(512 + 256 * t - 1280))
+        aff(sf("T4", 16 * t, 16 * t + 16, k=4), sf("cdm"), 1.0, float(768 + 1280 - 512 + 256 * t))
+        if t > 0:
+            aff(sf("c2"), cur(t), 2.0, 2.0)
+
+    def spawn_block(t):
+        o = P(5, 0, 256)
+        mm(([(o, sq("dg4"), LP)] if t < 2 else []) + ids(o, 256))
+        act(R("SP", 512 + 256 * t, 768 + 256 * t), o, AF.Identity, bias=col("bs", t) if t < 2 else col("b4", t))
+
+    def constants_1():
+        aff(Ft("j17", 17, 34), Ft("j17", 0, 17), 1.0, pm)
+        aff(Ft("j17", 34, 51), Ft("j17", 17, 34), -16.0, 256.0)
+        aff(sf("dum"), sf("lane"), 1.0, 1280.0)
+        aff(cur(0), sf("lane"))
+        ts(Jt("x17", 0, 17), Ft("j17", 17, 34), 8.0, AL.subtract, 1.0 / 17, AL.mult)
+        ts(Jt("a", 256, 272), sf("lane"), 2048.0, AL.add)
+        ts(Ft("j17", 51, 68), Jt("x17", 0, 17), 273.0, AL.mult)
+        tt(Ft("j17", 68, 85), Ft("j17", 34, 51), Ft("j17", 51, 68), AL.add)
+        cp(su("Lp", 0, 17, k=2), Ft("j17", 68, 85))
+
+    def constants_2():
+        aff(cf("nth", k=3), R("thb", 0, 3), -1.0, 0.5)
+        aff(cf("t7"), col("q", 1), 1.0, col("oh", 8))
+        aff(cf("p4"), col("q", 0), 1.0, cf("t7"))
+        aff(cf("dl"), col("oh", 3), -1.0, col("oh", 1))
+        aff(Mt("dg4"), Mt("eye"), cf("p4"))
+        aff(cf("b3", k=3), sf("c1", 0, 3), 256.0, 512.0)
+        aff(cf("b4", k=3), cf("b3"), col("oh", 4))
+        for t in range(2):
+            aff(cf("bs", t, t + 1, k=2), cf("dl"), 0.5 ** (t + 1), col("b4", t))
+        onehot(sq("bd"), Ft("tmp", 0, 128), Ft("k", 0, 128), col("nb", 2))
+        aff(sf("l16"), sf("lane"), 1.0 / 16)
+        aff(sf("l8"), sf("lane"), 8.0)
+        aff(cf("rs2"), col("oh", 6), -1.5, 1.0)
+        aff(cf("rb2"), col("oh", 6), 3.0)
+
+    def constants_3():
+        aff(cf("t8"), pm, 4096.0, 4096.0)
+        aff(cf("t9"), pm, -256.0)
+        act(Bt("nt"), Ft("y", 0, 256), AF.Relu, bias=cf("t8"), scale=-4096.0)
+        aff(cf("wi1"), col("q", 2), 1.0, col("oh", 8))
+        aff(sq("bdid"), sq("bd"), cf("wi1"))
+        act(Bt("nm"), Ft("y", 0, 256), AF.Abs, bias=cf("t9"), scale=256.0)
+        act(Bt("rst"), Ft("y", 0, 256), AF.Relu, bias=8192.0, scale=-8192.0)
+
+    def constants_4():
+        aff(cf("m4"), col("oh", 8), -4.0)
+        aff(cf("weh", k=2), cf("q", 0, 2), 1.0, cf("m4"))
+        for i, nm in enumerate(("e", "h")):
+            aff(Mt(nm), Mt("one"), col("weh", i))
+            to_list(P(1, 32 * i, 32 * i + 32), nm, R("SP", 0, 512))
+        cp(su("eh", k=4), P(1, 0, 64))
+
+    def inverse(i):
+        for h in range(2):
+            cp(IX(R("SE", 512 * i, 512 * i + 512), su("eh", 32 * i + 16 * h, 32 * i + 16 * h + 16)), R("SP", 256 * h, 256 * h + 256))
+        to_list(P(1, 0, 32), "id", R("SE", 512 * i, 512 * i + 512))
+        cp(su("inv", 32 * i, 32 * i + 32, k=4), P(1, 0, 32))
+
+    def constants_6():
+        aff(cf("sg"), col("oh", 1), -1.0, col("oh", 0))
+        aff(cf("sg1"), cf("sg"), -1.0, -1.0)
+        for i, o in enumerate((512.0, 256.0, 0.0)):
+            aff(sf("D4", 16 * i, 16 * i + 16), sf("lane"), 1.0, o)
+        aff(sf("T4", 48, 64), sf("lane"), 1.0, -256.0)
+        aff(sp(3), sp(0))
+        aff(sf("l8b", 0, 8), sf("l8", 0, 8))
+        aff(sf("l8b", 8, 16), sf("l8", 8, 16), 1.0, -1024.0)
+
+    def constants_5():
+        for i in range(2):
+            aff(R("MK", 512 * i, 512 * i + 512), R("S2", 0, 512), col("oh", i))
+        aff(R("RR", 0, 768), R("S1", 0, 768), cf("sg1"))
+
+    constants_1()
+
+    for t in range(NR):
+        land = "land%d" % t
+        for c in range(4):
+            act(R("G", 1024 * c, 1024 * c + 1024), IX(R("PT", 0, 2048), su("tile", 64 * c, 64 * c + 64)), AF.Copy)
+            to_list(P(0, 64 * c, 64 * c + 64), "key", R("G", 1024 * c, 1024 * c + 1024))
+        na = NA[t]
+        n2 = 16 - na - NTAIL
+
+        def cand(k, w=1):
+            return IX(R("XE", 0, 2048), su("tile", 16 * k, 16 * (k + w)))
+
+        for k in range(n2):
+            if k < 2:
+                cp(Bt("mx%d" % k), cand(k))
+            else:
+                tt(Bt("mx%d" % (k % 4)), cand(k), Bt("mx%d" % ((k - 2) % 4)), AL.max)
+        if na:
+            act(Bt("xa", 0, 256 * na, k=3), cand(16 - na, na), AF.Copy)
+        if t == 0:
+            codes()
+            pre(0)
+            constants_2()
+            spawn_block(0)
+            cp(su("Lx"), sf("c1"))
+        if t == 1:
+            to_list(P(6, 0, 128), "id", R("PT", 0, 2048))
+            constants_6()
+        if t == 2:
+            constants_5()
+        parts = [Bt("xa", 256 * j, 256 * j + 256) for j in range(na)] + [Bt("mx%d" % ((n2 - 2) % 4)), Bt("mx%d" % ((n2 - 1) % 4))]
+        total = [parts[0]]
+        for j, x in enumerate(parts[1:]):
+            mm([(P(7, 0, 256), sq("eye"), x)] + [(P(7, 0, 256), sq("neye"), u) for u in total])
+            act(Bt("mr%d" % j), P(7, 0, 256), AF.Relu)
+            total.append(Bt("mr%d" % j))
+        mm([(P(7, 0, 256), sq("eye"), u) for u in total])
+        top = R("VE", 1536, 1792)
+        act(Bt("mt0") if NTAIL else top, P(7, 0, 256), AF.Copy)
+        for j in range(NTAIL):
+            tt(top if j == NTAIL - 1 else Bt("mt%d" % ((j + 1) % 2)), cand(n2 + j), Bt("mt%d" % (j % 2)), AL.max)
+        tt(Jt("v", 0, 256), P(0, 0, 256), Ft("cb", 0, 256), AL.subtract)
+        ts(Jt("tb"), IX(Jt("v"), su("Lp", 0, 17)), 11, AL.arith_shift_right, 0x1001 | (1 << 20), AL.bitwise_and)
+        ts(Jt("nn"), Jt("tb"), 1.0 / 4096, AL.mult, 0.5 - 1.0 / 8192, AL.add)
+        ts(Ft("nh"), Jt("nn"), 1.0, AL.not_equal)
+        scan(Ft("sc"), Ft("nh"), Ft("code"), 4194304.0, AL.mult, AL.max)
+        cp(si("s"), Ft("sc", 16, 272, 17))
+        ts(si("al"), si("s"), 4095, AL.bitwise_and)
+        cp(su("al"), si("al"))
+        act(Bt("gf"), IX(R("PT"), su("al")), AF.Copy)
+        to_list(P(1, 0, 16), "id", Bt("gf"))
+        act(Bt("xf"), IX(R("XE"), su("al")), AF.Copy)
+        ts(sf("nr"), si("al"), 2048.0, AL.is_ge)
+        tt(sf("tq"), sf("nr"), sf("cm"), AL.mult)
+
+        def same_strand(xs):
+            for x in xs:
+                w = 240 - 16 * x
+                o = R("EQ", 256 * (x + 1), 256 * (x + 1) + w)
+                ts(o, su("curR", 256 - w, 256, k=16), sf("key", x, x + 1), AL.is_equal)
+                mm([(P(0, 256 - w, 256), sq("bd"), o)], first=False, last=(x == 14))
+
+        if t > 0:
+            ts(sf("pm5"), si("al"), 2048.0, AL.is_ge, 0.5, AL.subtract)
+            tt(sf("key"), sf("pm5"), sf("c2"), AL.mult)
+            tt(R("EQ", 0, 256), IX(sf("key"), su("Lx")), Ft("curM", 0, 256), AL.is_equal)
+            mm([(P(0, 0, 256), sq("eye"), Bt("nm")), (P(0, 0, 256), sq("bd"), R("EQ", 0, 256))], last=False)
+            same_strand(range(0, 2))
+        if t == 1:
+            cp(su("Wl"), P(6, 0, 128))
+        tt(sf("sl"), P(1, 0, 16), sf("tq"), AL.add)
+        cp(su("sl"), sf("sl"))
+        tt(Bt("df"), IX(R("VE"), su("sl")), Bt("xf"), AL.subtract)
+        yn = R(land, 0, 256)
+        act(yn, Bt("df"), AF.Abs)
+        trs = []
+        for (d, sl_, engs) in first_hop(rank):
+            rid, pid = topo.addr(d, core)
+            trs.append(RemoteDMATransfer(dst_ids=[DstId(rid=rid, pnc=pid)], dma_engine_mask=bits(engs), remote_sem=sem["arr%d" % t],
+                                         src=yn[0], dst=T[land][:, 256 * sl_:256 * sl_ + 256]))
+            cnt["sent"] = cnt.get("sent", 0) + len(engs)
+        emit("g", lambda trs=trs: g.remote_dma_fused(trs, local_sem=sem["sent"]), [R(land, 256, 2048)], [yn],
+             kind="arr%d" % t, time=0.5, late=T_EXCH)
+        act(Bt("gs"), yn, AF.Sign, bias=col("nth", t))
+        if t > 0:
+            same_strand(range(2, 15))
+        to_list(P(3, 0, 16), "one", Bt("gs"))
+        to_list(P(2, 0, 16), "mark", yn)
+        if t > 0:
+            scan(Ft("sc", 0, 256), Bt("rst"), P(0, 0, 256), 0.0, AL.add, AL.min)
+            ts(sf("l0"), Ft("sc", 15, 256, 16), 0.0, AL.is_equal)
+            tt(sf("lead"), sf("l0"), sf("nr"), AL.mult)
+            lead = sf("lead")
+        else:
+            lead = sf("nr")
+        tt(sf("u3"), sf("cdm"), lead, AL.mult)
+        ts(sf("wl"), P(3, 0, 16), 2.0, AL.is_ge)
+        tt(sf("u4"), sf("u3"), sf("dum"), AL.add)
+        tt(sp(t), sf("wl"), lead, AL.mult)
+        tt(sf("a1"), sp(t), sf("dn"), AL.mult)
+        nxt = cur(t + 1) if t < 2 else sf("last")
+        tt(sf("vo"), sf("u4"), sf("a1"), AL.add)
+        tt(nxt, P(1, 0, 16), sf("a1"), AL.add)
+        cp(su("vo"), sf("vo"))
+        cp(su("nc"), nxt)
+        cp(IX(R("VE", 0, 1536), su("vo")), yn)
+
+        def zlist():
+            ts(si("d"), si("u"), 0x70, AL.bitwise_and)
+            tt(sf("zz"), si("d"), sf("l16"), AL.add)
+            ts(su("zl"), sf("zz"), 16.0, AL.mult)
+
+        def cells_of_arrivals(base):
+            cp(si("mz"), P(2, 0, 16))
+            ts(si("m7"), si("mz"), 7, AL.bitwise_and)
+            tt(sf("bo"), si("m7"), sf(base), AL.add)
+            cp(su("bo"), sf("bo"))
+
+        if t < 2:
+            nv = 768 + 256 * t
+            aff(Bt("rb", 0, 16), sf("nr"), -1.0, 1.0)
+            mm([(P(7, 0, 16), sq("bd"), Bt("rb", 0, 16))])
+            act(R("XE", 2048, 2304), yn, AF.Copy)
+            act(sf("tmp"), P(7, 0, 16), AF.Identity, acc=cf("A"))
+            act(LP, IX(R("SP", 0, nv), su("nc")), AF.Copy)
+            for c in range(NDV):
+                greater_v(c, nv)
+            for c in range(NDV, 4):
+                fetch_a(c, nv)
+            act(Bt("vc"), IX(R("VE", 0, nv), su("nc")), AF.Copy)
+            for c in range(NDV):
+                count(c, False)
+            for c in range(NDV, 4):
+                greater_a(c)
+            tile(t + 1)
+            zlist()
+            codes()
+            for c in range(NDV, 4):
+                count(c, True)
+            if t == 0:
+                constants_3()
+                constants_4()
+            inverse(t)
+            mm([(P(0, 0, 256), sq("bdid"), LP)])
+            cp(su("curR", k=16), P(0, 0, 256))
+            act(Bt("z"), IX(R(land), su("zl")), AF.Copy)
+            tt(Bt("g2"), IX(R(land), su("zl")), Bt("vc"), AL.is_lt)
+            to_list(P(2, 0, 16), "mark", Bt("z"))
+            mm([(P(6, 0, 256), sq("dg"), LP), (P(6, 0, 256), Mt("one", 9, 137), Bt("g2"))])
+            act(Bt("lpb"), P(6, 0, 256), AF.Relu, bias=cf("rb"), scale=cf("rs"))
+            pre(t + 1)
+            cells_of_arrivals("l8")
+            cp(IX(R("PT", 0, 2048), su("bo")), Bt("lpb"))
+            cp(IX(R("XE", 0, 2048), su("bo")), Bt("z"))
+            lane_keys()
+            mm([(P(1, 0, 256), sq("bdid"), LP), (P(1, 0, 256), sq("eye"), Bt("nt"))])
+            act(Ft("curM", 0, 256), P(1, 0, 256), AF.Copy)
+            spawn_block(t + 1)
+        else:
+            act(LP, IX(R("SP"), su("nc")), AF.Copy)
+            store("s", T.yv[:], R("VE", 0, 1280))
+            tt(sf("T4"), sf("T4"), sf("sp"), AL.mult)
+            cp(si("m"), P(2, 0, 16))
+            tt(sf("T4"), sf("T4"), sf("D4"), AL.add)
+            ts(si("u"), si("m"), 4095, AL.bitwise_and)
+            cp(su("l4", k=4), sf("T4"))
+            zlist()
+            l0, l1, l2, z0 = [su("l4", 16 * i, 16 * i + 16) for i in range(4)]
+            cp(IX(R("S2"), l2), Bt("two"))
+            act(Bt("g1"), IX(R("S2"), l1), AF.Copy)
+            cp(R("S1", 768, 1536), R("S2", 768, 1536))
+            act(Bt("z"), IX(R(land), su("zl")), AF.Copy)
+            to_list(P(2, 0, 16), "mark", Bt("z"))
+            tt(IX(R("S1"), l1), Bt("g1"), R("S2", 1536, 1792), AL.add)
+            aff(Ft("q1", 0, 256), Bt("g1"), cf("sg"))
+            act(Ft("q0", 0, 256), IX(R("S1"), l0), AF.Identity, scale=cf("sg"))
+            act(R("S0", 256, 512), R("S1", 1024, 1280), AF.Copy)
+            tt(R("S0", 0, 256), IX(R("S1", 1280, 1552), z0), R("S1", 768, 1024), AL.add)
+            for i in range(2):
+                act(R("SE", 512 * i, 512 * i + 512), IX(R("S0"), su("inv", 32 * i, 32 * i + 32)), AF.Copy)
+            cells_of_arrivals("l8b")
+            for h in range(2):
+                cp(IX(R("XE", 1024 * h, 1024 * h + 1024), su("bo", 8 * h, 8 * h + 8)), Bt("z", 128 * h, 128 * h + 128))
+                store("s", T.yx[:, 1024 * h:1024 * h + 1024], R("XE", 1024 * h, 1024 * h + 1024))
+            scan(R("CE", 1, 513), R("SE", 0, 512), R("MK", 0, 512), 0.0, AL.add, AL.mult)
+            act(R("RA"), IX(R("CE", 0, 513), su("eh", 0, 32)), AF.Copy)
+            for h in range(2):
+                cp(IX(R("PT", 1024 * h, 1024 * h + 1024), su("bo", 8 * h, 8 * h + 8)), R("PT", 2048 + 128 * h, 2176 + 128 * h))
+                mm([(P(6, 0, 128), Mt("id", 15 - y, 143 - y), R("PT", 128 * y, 128 * y + 128)) for y in range(8 * h, 8 * h + 8)],
+                   first=(h == 0), last=(h == 1))
+            act(Ft("wo", 0, 128), P(6, 0, 128), AF.Copy)
+            store("a", T.yw[:], Ft("wo", 0, 128))
+            scan(R("CE", 528, 1040), R("SE", 512, 1024), R("MK", 512, 1024), -1.0, AL.add, AL.mult)
+            tt(R("RR", 768, 1280), IX(R("CE", 528, 1040), su("eh", 32, 64)), R("RA"), AL.add)
+            tt(R("RR", 1280, 1536), IX(R("RR", 0, 1280), l0), Ft("q0", 0, 256), AL.add)
+            tt(R("RR", 1536, 1792), IX(R("RR", 0, 1536), l1), Ft("q1", 0, 256), AL.add)
+            ts(R("RR", 1792, 2048), IX(R("RR", 0, 1792), l2), cf("sg"), AL.add)
+            store("s", T.ye[:], R("RR", 768, 2048, p=(0, 128, 16)))
+            store("a", T.yh[:], R("RR", 768, 2048, p=(1, 128, 16)))
+
+    issue()

@@ -5,16 +5,26 @@ AL = AluOpType
 AF = ActivationFunctionType
 NR = 3
 NDV = 2
-T_CYCLE, T_CALL, T_WAKE, T_LOOK, T_PE, T_DMA, T_EXCH = 0.001, 0.05, 0.06, 0.5, 0.0005, 2.0, 9.5
-T_GATHER, T_SCATTER = 1.56, 3.8
-PASSES, SHAKE, SEED = 600, 0.5, 4
-NA = [0, 2, 2]
-NTAIL = 0
+T_CALL, T_INDIRECT, T_WAKE, T_LOOK, T_PE, C_PE, T_DMA = 0.015, 0.055, 0.05, 0.5, 0.58, 4, 1.9
+T_ROW, T_BYTE = 0.02, 0.00005
+T_EXCH = [9.5, 7.0, 7.0]
+GATE = False
+PACES = [(0.00097, 1.56, 3.8, 0.05, 0.85, 1.0, 1.0), (0.00087, 1.3, 2.5, 0.1, 1.3, 1.2, 1.1), (0.0012, 1.9, 5.0, 0.06, 1.1, 0.9, 1.2),
+         (0.001, 1.3, 5.0, 0.03, 0.75, 1.2, 0.9)]
+PASSES, SWAPS, SHAKE, SEED, HEAT = 15, 32000, 0.5, 3, 0.012
+NA = [4, 4, 4]
+NP = [1, 1, 1]
+NCV = 0
+CUT = 4
+IDS, PEDF, SILU, G2A, SHORT, WROW = False, 0, [1], False, False, False
+INV = [[0, 1], []]
 ORDER = {}
 
 SCRATCH = {
     "XE": ("sbuf", [128, 2304], "bfloat16"),
-    "VE": ("sbuf", [128, 1792], "bfloat16"),
+    "VE": ("sbuf", [128, 3584], "bfloat16"),
+    "PC": ("sbuf", [128, 2048], "bfloat16"),
+    "RS": ("sbuf", [128, 2048], "bfloat16"),
     "PT": ("sbuf", [128, 2304], "bfloat16"),
     "SP": ("sbuf", [128, 1280], "bfloat16"),
     "G": ("sbuf", [128, 4096], "bfloat16"),
@@ -25,22 +35,23 @@ SCRATCH = {
     "land1": ("sbuf", [128, 2048], "bfloat16"),
     "land2": ("sbuf", [128, 2048], "bfloat16"),
     "B": ("sbuf", [128, 7680], "bfloat16"),
-    "F": ("sbuf", [128, 5440], "float32"),
+    "F": ("sbuf", [128, 6528], "float32"),
     "J": ("sbuf", [128, 2448], "int32"),
-    "M": ("sbuf", [128, 2592], "bfloat16"),
+    "M": ("sbuf", [128, 2880], "bfloat16"),
     "sf": ("sbuf", [128, 1024], "float32"),
     "si": ("sbuf", [128, 320], "int32"),
     "su": ("sbuf", [128, 1152], "uint16"),
     "cf": ("sbuf", [128, 112], "float32"),
     "thb": ("sbuf", [128, 8], "bfloat16"),
-    "EH": ("sbuf", [128, 512], "int32"),
-    "EA": ("sbuf", [128, 1024], "bfloat16"),
-    "IH": ("sbuf", [128, 1024], "bfloat16"),
-    "S2": ("sbuf", [128, 1792], "bfloat16"),
-    "S1": ("sbuf", [128, 1552], "bfloat16"),
+    "EH": ("sbuf", [128, 128], "int32"),
+    "EA": ("sbuf", [128, 128], "bfloat16"),
+    "ZS": ("sbuf", [128, 512], "bfloat16"),
+    "Z0": ("sbuf", [128, 144], "float32"),
+    "WF": ("sbuf", [128, 2048], "float32"),
+    "S2": ("sbuf", [128, 1808], "float32"),
     "S0": ("sbuf", [128, 512], "bfloat16"),
     "SE": ("sbuf", [128, 1024], "bfloat16"),
-    "MK": ("sbuf", [128, 1024], "bfloat16"),
+    "MK": ("sbuf", [128, 512], "bfloat16"),
     "CE": ("sbuf", [128, 1040], "float32"),
     "RA": ("sbuf", [128, 512], "float32"),
     "RR": ("sbuf", [128, 2048], "float32"),
@@ -48,7 +59,7 @@ SCRATCH = {
 for _i in range(8):
     SCRATCH["p%d" % _i] = ("psum", [128, 512], "float32")
 
-SEMAPHORES = ["cv", "ca", "ct", "cg", "sent"] + ["arr%d" % _i for _i in range(NR)] + ["d%d" % _i for _i in range(20)]
+SEMAPHORES = ["cv", "ca", "ct", "cg", "sent"] + ["arr%d" % _i for _i in range(NR)] + ["d%d" % _i for _i in range(24)]
 
 
 def routes(T, topo):
@@ -138,7 +149,9 @@ def rank_program(g, core, T, topo):
             Q[e].wait_ge(sem[tok[0]], tok[1])
             known[e][tok[0]] = tok[1]
 
-    def emit(e, fn, outs, ins, kind="c", rate=1.0, time=None, late=0.0):
+    gate = []
+
+    def emit(e, fn, outs, ins, kind="c", rate=1.0, time=None, cycles=0, late=0.0):
         wr, rd = [], []
         full = [x for x in ins if isinstance(x, tuple)]
         for o in outs:
@@ -146,19 +159,19 @@ def rank_program(g, core, T, topo):
             rd += o[2]
         for i in full:
             rd += i[1] + i[2]
-        if time is None:
-            o = outs[0]
-            if o[2]:
-                cyc = T_SCATTER * o[3]
-            elif any(i[2] for i in full):
-                cyc = T_GATHER * o[3]
-            else:
-                if rate == 0.5 and not (o[4] and all(i[4] for i in full if i[3] > 1)):
-                    rate = 1.0
-                cyc = max(64.0, rate * max([o[3]] + [i[3] for i in full]))
-            time = T_CALL + cyc * T_CYCLE
+        if time is not None:
+            cost = (time, cycles, 0, 0)
+        elif outs[0][2]:
+            cost = (T_INDIRECT, 0, 0, outs[0][3])
+        elif any(i[2] for i in full):
+            cost = (T_INDIRECT, 0, outs[0][3], 0)
+        else:
+            if rate == 0.5 and not (outs[0][4] and all(i[4] for i in full if i[3] > 1)):
+                rate = 1.0
+            cost = (T_CALL, max(64.0, rate * max([outs[0][3]] + [i[3] for i in full])), 0, 0)
+        time = cost[0] + PACES[0][0] * (cost[1] + PACES[0][1] * cost[2] + PACES[0][2] * cost[3])
         who = e if kind == "c" else "x%d" % len(nodes)
-        deps = set()
+        deps = set(gate)
         for w, regs in ((True, wr), (False, rd)):
             for (nm, a, b) in regs:
                 ps = SCRATCH[nm][0] == "psum"
@@ -166,7 +179,7 @@ def rank_program(g, core, T, topo):
                     if (ps and (e2 != e or e == "t")) or (a < b2 and a2 < b and (w or w2)):
                         deps.add(nd)
         me = len(nodes)
-        nodes.append({"e": e, "fn": fn, "kind": kind, "time": time, "late": late, "deps": deps})
+        nodes.append({"e": e, "fn": fn, "kind": kind, "time": time, "cost": cost, "late": late, "deps": deps})
         for (nm, a, b) in wr:
             ps = SCRATCH[nm][0] == "psum"
             recs[nm] = [x for x in recs.get(nm, []) if not (a <= x[0] and x[1] <= b) and not (ps and e == "t")]
@@ -185,17 +198,18 @@ def rank_program(g, core, T, topo):
         for i in range(m - 1, -1, -1):
             rest[i] = nodes[i]["time"] + nodes[i]["late"] + max([rest[k] + T_WAKE for k in kids[i]] + [0.0])
         pars = [sorted(nd["deps"]) for nd in nodes]
-        eng = [nd["e"] for nd in nodes]
+        eng = ["h" if "head" in nd else nd["e"] for nd in nodes]
+        names = list(Q) + ["h"]
 
         def plan(before, after, prio, back):
             left = [len(x) for x in before]
             at = [nodes[i]["late"] if back else 0.0 for i in range(m)]
-            ready = {e: [i for i in range(m) if left[i] == 0 and eng[i] == e] for e in Q}
-            free = {e: 0.0 for e in Q}
+            ready = {e: [i for i in range(m) if left[i] == 0 and eng[i] == e] for e in names}
+            free = {e: 0.0 for e in names}
             end = [0.0] * m
             seq = []
             for _ in range(m):
-                t1, e = min((min(max(at[i], free[e]) + nodes[i]["time"] for i in ready[e]), e) for e in Q if ready[e])
+                t1, e = min((min(max(at[i], free[e]) + nodes[i]["time"] for i in ready[e]), e) for e in names if ready[e])
                 t0 = max(min(at[i] for i in ready[e]), free[e])
                 i = max([j for j in ready[e] if at[j] <= t0 + T_LOOK * (t1 - t0)], key=lambda j: (prio[j], -j))
                 ready[e].remove(i)
@@ -209,22 +223,102 @@ def rank_program(g, core, T, topo):
                         ready[eng[k]].append(k)
             return max(end), end, seq
 
+        paces = [([nd["cost"][0] + c * (nd["cost"][1] * (pe if nd["e"] == "t" else 1.0) + ga * nd["cost"][2] + sc * nd["cost"][3]) for nd in nodes],
+                  [nd["late"] * (ex if nd["kind"][:3] == "arr" else dm) for nd in nodes], wk) for (c, ga, sc, wk, ex, pe, dm) in PACES]
+
+        def replay(seq, pace):
+            time, late, wake = pace
+            free = {e: (0.0, -1) for e in names}
+            end, start, why = [0.0] * m, [0.0] * m, [-1] * m
+            for i in seq:
+                t0, why[i] = free[eng[i]]
+                for d in pars[i]:
+                    if end[d] + wake > t0 and not (eng[d] == "t" and eng[i] == "t"):
+                        t0, why[i] = end[d] + wake, d
+                start[i] = t0
+                free[eng[i]] = (t0 + time[i], i)
+                end[i] = t0 + time[i] + late[i]
+            return max(end), start, why, end
+
+        def score(seq):
+            return sum(replay(seq, p)[0] / w for p, w in zip(paces, norm))
+
         if m not in ORDER:
             best = None
             prio = rest
-            x = SEED
+            rnd = [SEED]
+
+            def draw():
+                rnd[0] = (rnd[0] * 1103515245 + 12345) % 2147483648
+                return rnd[0] / 2147483648
+
             for _ in range(PASSES):
                 span, end, seq = plan(pars, kids, prio, False)
-                if best is None or span < best[0]:
-                    best = (span, seq, end)
-                end = list(best[2] if span > best[0] + 1.0 else end)
+                if best is None:
+                    norm = [replay(seq, p)[0] for p in paces]
+                val = score(seq)
+                if best is None or val < best[0]:
+                    best = (val, seq, end, span)
+                end = list(best[2] if span > best[3] + 1.0 else end)
                 for i in range(m):
-                    x = (x * 1103515245 + 12345) % 2147483648
-                    end[i] += SHAKE * x / 2147483648
+                    end[i] += SHAKE * draw()
                 prio = plan(kids, pars, end, True)[1]
-            ORDER[m] = best
+            val, seq = best[0], best[1]
+            kept = (val, seq)
+            for step in range(SWAPS):
+                if val < kept[0]:
+                    kept = (val, seq)
+                slack = 1e-9 + HEAT * (1 - step / SWAPS) ** 2 * draw() * draw()
+                span, start, why, end = replay(seq, paces[int(draw() * len(paces))])
+                seq = sorted(seq, key=lambda i: start[i])
+                chain = []
+                i = end.index(span)
+                while why[i] >= 0:
+                    if why[i] not in nodes[i]["deps"]:
+                        chain.append((why[i], i))
+                    i = why[i]
+                if not chain:
+                    continue
+                j, i = chain[int(draw() * len(chain))]
+                if draw() < 0.35:
+                    mine = [k for k in seq[:seq.index(i)] if eng[k] == eng[i]]
+                    j = mine[max(0, len(mine) - 1 - int(draw() * draw() * 10))]
+                    b = seq.index(j)
+                    a = b
+                    while a > 0 and seq[a - 1] not in nodes[j]["deps"]:
+                        a -= 1
+                    if a == b:
+                        continue
+                    a += int(draw() * (b - a))
+                    new = seq[:a] + [j] + seq[a:b] + seq[b + 1:]
+                    v = score(new)
+                    if v <= val + slack:
+                        val, seq = v, new
+                    continue
+                a, b = seq.index(j), seq.index(i)
+                early, rest_, moved = [], [], {j}
+                for k in seq[a + 1:b + 1]:
+                    if moved & nodes[k]["deps"]:
+                        moved.add(k)
+                        rest_.append(k)
+                    else:
+                        early.append(k)
+                if i in moved:
+                    continue
+                tail = []
+                for k in seq[b + 1:b + 1 + int(draw() * draw() * 40)]:
+                    if moved & nodes[k]["deps"]:
+                        break
+                    tail.append(k)
+                new = seq[:a] + early + tail + [j] + rest_ + seq[b + 1 + len(tail):]
+                v = score(new)
+                if v <= val + slack:
+                    val, seq = v, new
+            val, seq = min(kept, (val, seq))
+            ORDER[m] = (val, seq, [replay(seq, p)[0] for p in paces])
         tok = [None] * m
-        for i in ORDER[m][1]:
+        head = [i for i in range(m) if "head" in nodes[i]]
+        for i in head + [i for i in ORDER[m][1] if i not in head]:
             nd = nodes[i]
             e = nd["e"]
             toks = {}
@@ -270,7 +364,9 @@ def rank_program(g, core, T, topo):
         emit("v", lambda: g.vector.tensor_tensor_scan(out[0], d0[0], d1[0], init, op0, op1), [out], [d0, d1], rate=0.5)
 
     def act(out, in_, f, bias=0.0, scale=1.0, acc=None):
-        if acc is None:
+        if out[2]:
+            emit("a", lambda: g.scalar.activation(out[0], in_[0], f), [out], [in_])
+        elif acc is None:
             emit("a", lambda: g.scalar.activation(out[0], in_[0], f, bias=A_(bias), scale=A_(scale)), [out], [in_, bias, scale])
         else:
             emit("a", lambda: g.scalar.activation(out[0], in_[0], f, bias=A_(bias), scale=A_(scale), accum_out=acc[0]), [out, acc], [in_, bias, scale])
@@ -282,27 +378,36 @@ def rank_program(g, core, T, topo):
         act(tmp, in_, AF.Abs, bias=neg)
         act(out, tmp, AF.Relu, bias=1.0, scale=-1.0)
 
-    def mm(items, first=True, last=True):
+    def mm(items, first=True, last=True, wide=1):
         def fn():
             r_ = None
             for i, (o, l, r) in enumerate(items):
                 r_ = g.tensor.matmul(o[0], l[0], r[0], first and i == 0, last and i == len(items) - 1)
             return r_
         emit("t", fn, [x[0] for x in items], [x[1] for x in items] + [x[2] for x in items],
-             time=sum(max(64, x[2][3]) for x in items) * T_PE)
+             time=0.0, cycles=sum(max(64, x[2][3]) * T_PE * wide + C_PE for x in items))
 
     def iota(out, pat, base=0, cm=0):
         emit("g", lambda: g.iota(out[0], pat, base, cm, allow_small_or_imprecise_dtypes=True), [out], [],
-             time=0.13 + 2 * out[3] * T_CYCLE)
+             time=0.15, cycles=2 * out[3])
+
+    def memset(out, c):
+        emit("v", lambda: g.vector.memset(out[0], c), [out], [], rate=0.5)
 
     def fill(out, c):
         iota(out, [[0, out[3]]], c)
 
-    def load(e, out, src):
-        emit(e, lambda: Q[e].dma_start(out[0], src), [out], [], kind="dma", time=0.1, late=T_DMA + out[3] * 0.001)
+    landed = [T_DMA]
 
-    def store(e, dst, in_):
-        emit(e, lambda: Q[e].dma_start(dst, in_[0]), [], [in_], kind="dma", time=0.1, late=T_DMA + in_[3] * 0.001)
+    def load(e, out, src, rows, size):
+        landed[0] += rows * (T_ROW + size * T_BYTE)
+        nodes[emit(e, lambda: Q[e].dma_start(out[0], src), [out], [], kind="dma", time=0.0, late=landed[0])]["head"] = True
+
+    def store(e, dst, in_, rows, size):
+        emit(e, lambda: Q[e].dma_start(dst, in_[0]), [], [in_], kind="dma", time=0.1, late=T_DMA + rows * (T_ROW + size * T_BYTE))
+
+    def move(out, in_):
+        emit("s", lambda: g.sync.dma_start(out[0], in_[0]), [out], [in_], kind="dma", time=0.1, late=T_DMA + 0.5)
 
     def slots(buf, w):
         names = {}
@@ -324,6 +429,12 @@ def rank_program(g, core, T, topo):
         nm, a, b = src[1][0]
         mm([(out, Mt(z, 15 - y, 143 - y), R(nm, a + y, b, 16)) for y in range(16)])
 
+    def to_list_short(name, bank, block, src):
+        mm([(P(bank, 0, 256), sq("eye"), Bt("nm"))], last=False)
+        mm([(P(bank, 0, 256), sq(block), src)], first=False)
+        scan(Ft(name, 0, 256), Bt("rst"), P(bank, 0, 256), 0.0, AL.add, AL.min)
+        return Ft(name, 15, 256, 16)
+
     def col(name, i):
         return cf(name, i, i + 1)
 
@@ -332,34 +443,41 @@ def rank_program(g, core, T, topo):
 
     LP = R("PT", 2048, 2304)
 
-    load("a", R("EH", p=(0, 8)), T.e0[:])
-    load("a", (T.EH[8:16, :], [("EH", 600, 601)], [], 512, False), T.h0[:])
-    load("s", Jt("wn", 0, 128), T.w0[:])
-    load("s", R("XE", 2048, 2304), T.v0[:, 0:256])
-    load("s", R("VE", 0, 512), T.v0[:])
-    load("s", R("XE", 0, 2048), T.x0[:])
-    load("s", R("thb", 0, 3), T.th[:])
-    EHall = (T.EH[0:16, :], [("EH", 0, 601)], [], 512, False)
+    def quarter(name, i):
+        return (T[name][32 * i:32 * i + 32, :], [(name, 200 + i, 201 + i)], [], 128, name == "EA")
+
+    def whole(name):
+        return (T[name][:, :], [(name, 0, 204)], [], 128, name == "EA")
+
+    for i, src in enumerate((T.e0, T.e0, T.h0, T.h0)):
+        load("sa"[i // 2], quarter("EH", i), src[:], 2, 512)
+    load("s", Jt("wn", 0, 128), T.w0[:], 8, 512)
+    load("a", R("VE", 0, 512), T.v0[:], 8, 1024)
+    for h in range(2):
+        load("s", R("XE", 1024 * h, 1024 * h + 1024), T.x0[:, 1024 * h:1024 * h + 1024], 8, 2048)
+    load("s", R("XE", 2048, 2304), T.v0[:, 0:256], 8, 512)
+    load("s", R("thb", 0, 3), T.th[:], 8, 6)
 
     iota(si("p", 0, 1), [[0, 1]], 0, 1)
     iota(sf("c1"), [[1, 16]])
     iota(Ft("n", 0, 144), [[1, 144]])
     iota(sf("l1"), [[16, 8], [0, 2]])
-    iota(Ft("y", 0, 256), [[0, 16], [1, 16]])
-    iota(R("IH", 0, 512, p=(0, 1)), [[8, 64], [0, 8]])
-    iota(R("IH", 512, 1024, p=(0, 1)), [[0, 64], [1, 8]])
+    iota(Bt("num"), [[1, 256]])
+    iota(R("ZS"), [[1, 4], [4, 8], [32, 16]], 0, -1)
     iota(Ft("k", 0, 256), [[1, 16], [0, 16]])
     iota(sf("c16"), [[16, 16]])
     iota(Ft("j17", 0, 17), [[16, 17]])
     iota(Ft("pr"), [[-4096, 272]], 272 * 4096)
     fill(Jt("v", 256, 272), 2048)
-    fill(R("VE", 512, 1792), 0)
-    fill(R("S2"), 1)
-    fill(R("S1", 0, 1536), 1)
-    fill(R("S1", 1536, 1552), 0)
-    fill(Bt("two"), 2)
-    fill(R("CE", 0, 8), 0)
-    fill(sf("D4", 48, 64, k=4), 256)
+    fill(R("VE", 512, 1536), 0)
+
+    def late_fills():
+        iota(Ft("y", 0, 256), [[0, 16], [1, 16]])
+        fill(R("S2", 0, 1792), 64)
+        fill(R("S2", 1792, 1808), 0)
+        fill(Ft("two", 0, 256), 128)
+        fill(R("CE", 0, 8), 0)
+        fill(sf("D4", 48, 64, k=4), 512)
 
     ts(si("p", 1, 2), si("p", 0, 1), 15, AL.bitwise_and)
     ts(si("p", 2, 3), si("p", 0, 1), 4, AL.arith_shift_right)
@@ -369,12 +487,10 @@ def rank_program(g, core, T, topo):
     ts(si("p", 6, 7), si("p", 0, 1), 1, AL.arith_shift_right, 7, AL.bitwise_and)
     cp(cf("b", 0, 7, k=8), si("p", 0, 7))
     pf, pm, gi, p7, g0, h8, pq = [col("b", i) for i in range(7)]
-    ts(cf("t2"), p7, 16.0, AL.mult, 1.0, AL.add)
     ts(cf("t0"), g0, 16.0, AL.mult, h8, AL.add)
-    ts(cf("t3"), h8, 2.0, AL.mult, cf("t2"), AL.add)
     ts(cf("t1"), p7, 32.0, AL.mult, cf("t0"), AL.add)
     ts(su("L1"), sf("l1"), pm, AL.add)
-    ts(Mt("selA"), Ft("n", 0, 144), cf("t3"), AL.is_equal)
+    ts(R("ZS"), R("ZS"), 0.0, AL.is_equal)
     ts(su("L2", 0, 8), sf("c1", 0, 8), 2.0, AL.mult, cf("t1"), AL.add)
     ts(cf("wm"), pm, 2.0, AL.mult, 1.0, AL.add)
     ts(cf("zt"), gi, 16.0, AL.mult, 15.0, AL.add)
@@ -387,9 +503,11 @@ def rank_program(g, core, T, topo):
     aff(cf("bias0"), col("oh", 1), 4.0, cf("t4"))
     onehot(Mt("eye"), Ft("tmp", 0, 144), Ft("n", 0, 144), col("nb", 0))
     aff(cf("pass"), col("oh", 6), -1.0, 1.0)
-    aff(cf("rs"), col("oh", 6), -2.0, 1.0)
-    aff(cf("rb"), col("oh", 6), 11.0)
-    act(Mt("sel"), Ft("y", 0, 144), AF.Relu, bias=-14.0)
+    aff(cf("rb"), col("oh", 6), -5.0)
+    aff(Mt("d5"), Mt("eye"), col("oh", 5))
+    aff(cf("bias1"), col("oh", 4), 256.0, cf("bias0"))
+    if IDS:
+        aff(Bt("prio"), Ft("k", 0, 256), 4096.0)
     aff(Mt("dg"), Mt("eye"), cf("pass"))
     onehot(cf("q", k=8), sf("tmp", 0, 8), sf("c1", 0, 8), col("nb", 6))
     act(Mt("one"), Mt("mark"), AF.Sign)
@@ -406,9 +524,8 @@ def rank_program(g, core, T, topo):
     def tile(t):
         cp(si("m"), P(2, 0, 16))
         ts(si("u"), si("m"), 4095, AL.bitwise_and)
-        cp(sf("uf"), si("u"))
-        tt(si("sq"), sf("uf"), sf("uf"), AL.mult)
-        tt(Ft("t1", 0, 256), IX(sf("uf"), su("Lb")), Ft("kap", 0, 256), AL.mult)
+        tt(si("sq"), si("u"), si("u"), AL.mult)
+        tt(Ft("t1", 0, 256), IX(si("u"), su("Lb")), Ft("kap", 0, 256), AL.mult)
         ts(si("sh"), si("sq"), 5, AL.arith_shift_right)
         ts(sf("base"), si("sh"), cf("A") if t > 0 else 0.0, AL.add)
         tt(Jt("s", 0, 256), IX(sf("base"), su("Lb")), Ft("t1", 0, 256), AL.add)
@@ -418,16 +535,14 @@ def rank_program(g, core, T, topo):
     def codes():
         tt(Ft("code"), IX(Jt("a"), su("Lp", 0, 17, k=2)), Ft("pr"), AL.add)
 
-    def ids(o, w):
-        return [(o, Mt("sel", 11, 139, p=(0, 1)), R("IH", 0, w, p=(0, 1))),
-                (o, Mt("sel", 10, 138, p=(0, 1)), R("IH", 512, 512 + w, p=(0, 1)))]
-
-    cp(R("EA", 0, 512, p=(0, 16)), EHall)
-    tt(R("EA", 512, 1024, p=(0, 16)), EHall, R("EA", 0, 512, p=(0, 16)), AL.subtract)
-    to_list(P(2, 0, 16), "mark", R("XE", 2048, 2304))
-    mm([(P(4, 0, 512), Mt("selA", 1, 129, p=(0, 16)), R("EA", 0, 512, p=(0, 16))),
-        (P(4, 0, 512), Mt("selA", 0, 128, p=(0, 16)), R("EA", 512, 1024, p=(0, 16)))] + ids(P(4, 0, 512), 512))
-    act(R("SP", 0, 512), P(4, 0, 512), AF.Identity, bias=cf("bias0"))
+    cp(whole("EA"), whole("EH"))
+    for i in (1, 3):
+        tt(quarter("EA", i), quarter("EH", i), quarter("EA", i), AL.subtract)
+    to_list(P(2, 0, 16), "mark", R("VE", 0, 256))
+    for h in range(2):
+        mm([(P(4 + h, 0, 256), sq("d5"), Bt("num"))], last=False)
+        mm([(P(4 + h, 128 * j, 128 * j + 128), R("ZS", 256 * h + 128 * j, 256 * h + 128 * j + 128), whole("EA")) for j in range(2)], first=False)
+        act(R("SP", 256 * h, 256 * h + 256), P(4 + h, 0, 256), AF.Identity, bias=cf("bias%d" % h))
     cp(Ft("w2", 0, 256), IX(Jt("wn", 0, 128), su("L1")))
     emit("v", lambda: g.vector.transpose(Ft("w3", 0, 256)[0], Ft("w2", 0, 256)[0]), [Ft("w3", 0, 256)], [Ft("w2", 0, 256)])
     cp(su("Wl", k=8), IX(Ft("w3", 0, 256), su("L2", 0, 8)))
@@ -440,21 +555,24 @@ def rank_program(g, core, T, topo):
 
     def greater_v(c, nv):
         a, b, l = blk(c)
-        tt(R("GT", a, b), IX(R("VE", 0, nv), l), R("XE", a, b), AL.is_gt)
+        tt(R("GT", a, b), IX(R("VE", 0, nv), l), R("XE", a, b), AL.is_le)
 
     def fetch_a(c, nv):
         a, b, l = blk(c)
         act(R("VW", a, b), IX(R("VE", 0, nv), l), AF.Copy)
-        mm([(P(6 + c % 2, 0, 512), sq("eye"), R("VW", a, b)), (P(6 + c % 2, 0, 512), sq("neye"), R("XE", a, b))])
+        mm([(P(6 + c % 2, 0, 512), sq("neye"), R("VW", a, b)), (P(6 + c % 2, 0, 512), sq("eye"), R("XE", a, b))])
 
     def greater_a(c):
         a, b, l = blk(c)
-        act(R("GT", a, b), P(6 + c % 2, 0, 512), AF.Sign, bias=-0.5)
+        act(R("GT", a, b), P(6 + c % 2, 0, 512), AF.Sign, bias=0.5)
 
-    def count(c, signs):
+    def count(c, signs, vec=False):
         a, b, l = blk(c)
         mm([(P(4 + c % 2, 0, 512), sq("dg"), R("PT", a, b)), (P(4 + c % 2, 0, 512), Mt("one", 9, 137), R("GT", a, b))])
-        act(R("PT", a, b), P(4 + c % 2, 0, 512), AF.Relu, bias=cf("rb2" if signs else "rb"), scale=cf("rs2" if signs else "rs"))
+        if vec:
+            ts(R("PT", a, b), P(4 + c % 2, 0, 512), cf("rb"), AL.add, 0.0, AL.max)
+        else:
+            act(R("PT", a, b), P(4 + c % 2, 0, 512), AF.Relu, bias=cf("rb2" if signs else "rb"))
 
     def lane_keys():
         to_list(P(3, 0, 16), "key", LP)
@@ -463,7 +581,7 @@ def rank_program(g, core, T, topo):
 
     for c in range(4):
         greater_v(c, 512)
-        count(c, False)
+        count(c, False, c >= 4 - NCV)
     tile(0)
     lane_keys()
 
@@ -475,7 +593,6 @@ def rank_program(g, core, T, topo):
 
     def pre(t):
         tt(sf("cdm"), cur(t), sf("dum"), AL.subtract)
-        aff(sf("cm"), sf("cdm"), -1.0, 256.0)
         aff(sf("dn"), sf("cdm"), -1.0, float(512 + 256 * t - 1280))
         aff(sf("T4", 16 * t, 16 * t + 16, k=4), sf("cdm"), 1.0, float(768 + 1280 - 512 + 256 * t))
         if t > 0:
@@ -483,7 +600,7 @@ def rank_program(g, core, T, topo):
 
     def spawn_block(t):
         o = P(5, 0, 256)
-        mm(([(o, sq("dg4"), LP)] if t < 2 else []) + ids(o, 256))
+        mm(([(o, sq("dg4"), LP)] if t < 2 else []) + [(o, sq("d5"), Bt("num"))])
         act(R("SP", 512 + 256 * t, 768 + 256 * t), o, AF.Identity, bias=col("bs", t) if t < 2 else col("b4", t))
 
     def constants_1():
@@ -510,17 +627,26 @@ def rank_program(g, core, T, topo):
         onehot(sq("bd"), Ft("tmp", 0, 128), Ft("k", 0, 128), col("nb", 2))
         aff(sf("l16"), sf("lane"), 1.0 / 16)
         aff(sf("l8"), sf("lane"), 8.0)
-        aff(cf("rs2"), col("oh", 6), -1.5, 1.0)
-        aff(cf("rb2"), col("oh", 6), 3.0)
+        aff(cf("rb2"), col("oh", 6), 5.0)
 
     def constants_3():
-        aff(cf("t8"), pm, 4096.0, 4096.0)
-        aff(cf("t9"), pm, -256.0)
-        act(Bt("nt"), Ft("y", 0, 256), AF.Relu, bias=cf("t8"), scale=-4096.0)
+        memset(sf("hf"), 0.5)
+        scan(sf("pw"), sf("hf"), sf("hf"), 1.0, AL.mult, AL.mult)
+        tt(sf("hf"), sf("pw"), cf("oh"), AL.mult)
+        act(sf("pw"), sf("hf"), AF.Identity, acc=cf("w4"))
+        aff(cf("t9"), pm, -65536.0)
+        if SHORT or WROW:
+            aff(sq("bdq"), sq("bd"), col("q", 2))
+        if SHORT:
+            aff(sq("bdm"), sq("bd"), cf("wm"))
+        aff(sq("bdw"), sq("bd"), cf("w4"))
+        aff(cf("thr"), cf("w4"), 2.0)
         aff(cf("wi1"), col("q", 2), 1.0, col("oh", 8))
         aff(sq("bdid"), sq("bd"), cf("wi1"))
-        act(Bt("nm"), Ft("y", 0, 256), AF.Abs, bias=cf("t9"), scale=256.0)
-        act(Bt("rst"), Ft("y", 0, 256), AF.Relu, bias=8192.0, scale=-8192.0)
+        act(Bt("nm"), Ft("y", 0, 256), AF.Abs, bias=cf("t9"), scale=65536.0)
+        fill(Bt("rst"), 0)
+        emit("g", lambda: g.affine_select(Bt("rst")[0], Bt("rst")[0], [[0, 16], [1, 16]], AL.is_gt, 2097152.0, 0, 0),
+             [Bt("rst")], [Bt("rst")], time=0.2, cycles=512)
 
     def constants_4():
         aff(cf("m4"), col("oh", 8), -4.0)
@@ -531,102 +657,148 @@ def rank_program(g, core, T, topo):
         cp(su("eh", k=4), P(1, 0, 64))
 
     def inverse(i):
+        if i not in SILU:
+            for h in range(2):
+                cp(IX(R("SE", 512 * i, 512 * i + 512), su("eh", 32 * i + 16 * h, 32 * i + 16 * h + 16)), R("SP", 256 * h, 256 * h + 256))
+            to_list(P(1, 0, 32), "id", R("SE", 512 * i, 512 * i + 512))
+            cp(su("inv", 32 * i, 32 * i + 32, k=4), P(1, 0, 32))
+            return
+        if i == SILU[0]:
+            iota(R("RA"), [[1, 512]], 64)
+            aff(R("Z0"), Mt("one"), col("oh", 0))
+        a = 1024 + 512 * i
         for h in range(2):
-            cp(IX(R("SE", 512 * i, 512 * i + 512), su("eh", 32 * i + 16 * h, 32 * i + 16 * h + 16)), R("SP", 256 * h, 256 * h + 256))
-        to_list(P(1, 0, 32), "id", R("SE", 512 * i, 512 * i + 512))
-        cp(su("inv", 32 * i, 32 * i + 32, k=4), P(1, 0, 32))
+            act(IX(R("WF", a, a + 512), su("eh", 32 * i + 16 * h, 32 * i + 16 * h + 16)), R("RA", 256 * h, 256 * h + 256), AF.Silu)
+            if i == SILU[0] and h == 0:
+                nd = nodes[-1]
+                nd["cost"] = (nd["cost"][0], 1570, 0, nd["cost"][3])
+                nd["time"] += 1.5
+        mm([(P(1, 0, 32), R("Z0", 15 - y, 143 - y), R("WF", a + y, a + 512, 16)) for y in range(16)], wide=4)
+        ts(su("inv", 32 * i, 32 * i + 32, k=4), P(1, 0, 32), 64.0, AL.subtract)
 
     def constants_6():
         aff(cf("sg"), col("oh", 1), -1.0, col("oh", 0))
-        aff(cf("sg1"), cf("sg"), -1.0, -1.0)
+        aff(cf("sg64"), cf("sg"), 1.0 / 64)
+        aff(cf("oh64", k=2), cf("oh", 0, 2), 1.0 / 64)
         for i, o in enumerate((512.0, 256.0, 0.0)):
             aff(sf("D4", 16 * i, 16 * i + 16), sf("lane"), 1.0, o)
-        aff(sf("T4", 48, 64), sf("lane"), 1.0, -256.0)
+        aff(sf("T4", 48, 64), sf("lane"), 1.0, -512.0)
         aff(sp(3), sp(0))
-        aff(sf("l8b", 0, 8), sf("l8", 0, 8))
-        aff(sf("l8b", 8, 16), sf("l8", 8, 16), 1.0, -1024.0)
+        aff(sf("l8b", 0, CUT), sf("l8", 0, CUT))
+        aff(sf("l8b", CUT, 16), sf("l8", CUT, 16), 1.0, -128.0 * CUT)
 
     def constants_5():
-        for i in range(2):
-            aff(R("MK", 512 * i, 512 * i + 512), R("S2", 0, 512), col("oh", i))
-        aff(R("RR", 0, 768), R("S1", 0, 768), cf("sg1"))
+        gate.append(made)
+        fill(R("MK"), 1)
+        fill(R("RR", 0, 768), 0)
+        fill(R("WF", 0, 768), -2)
+        gate.pop()
+        move(R("RR", 0, 768, p=(0, 128, 16)), R("WF", 0, 768, p=(0, 8)))
 
     constants_1()
 
     for t in range(NR):
         land = "land%d" % t
         for c in range(4):
-            act(R("G", 1024 * c, 1024 * c + 1024), IX(R("PT", 0, 2048), su("tile", 64 * c, 64 * c + 64)), AF.Copy)
+            k0, k1 = 4 * c, 4 * c + 4
+            if c == 0 and NP[t]:
+                cp(R("G", 0, 256 * NP[t]), IX(R("PT", 0, 2048), su("tile", 0, 16 * NP[t])))
+                k0 = NP[t]
+            if k0 < k1:
+                act(R("G", 256 * k0, 256 * k1), IX(R("PT", 0, 2048), su("tile", 16 * k0, 16 * k1)), AF.Copy)
+        for c in ([1, 0, 2, 3] if NP[t] else range(4)):
             to_list(P(0, 64 * c, 64 * c + 64), "key", R("G", 1024 * c, 1024 * c + 1024))
+            o = P(1, 64 * c, 64 * c + 64)
+            if IDS:
+              mm([(o, sq("eye"), Bt("prio", 64 * c, 64 * c + 64))]
+               + [(o, Mt("id", 15 - y, 143 - y), R("G", 1024 * c + y, 1024 * c + 1024, 16)) for y in range(16)])
         na = NA[t]
-        n2 = 16 - na - NTAIL
+        n2 = 16 - na
+        np_ = na + 2
 
-        def cand(k, w=1):
-            return IX(R("XE", 0, 2048), su("tile", 16 * k, 16 * (k + w)))
+        def cand(k):
+            return IX(R("XE", 0, 2048), su("tile", 16 * k, 16 * k + 16))
+
+        def piece(j):
+            return (T.PC[:, j:256 * np_:np_], [("PC", 256 * j, 256 * j + 256)], [], 256, True)
 
         for k in range(n2):
+            o = piece(k - n2 + 2) if k >= n2 - 2 else Bt("mx%d" % (k % 4))
             if k < 2:
-                cp(Bt("mx%d" % k), cand(k))
+                cp(o, cand(k))
             else:
-                tt(Bt("mx%d" % (k % 4)), cand(k), Bt("mx%d" % ((k - 2) % 4)), AL.max)
-        if na:
-            act(Bt("xa", 0, 256 * na, k=3), cand(16 - na, na), AF.Copy)
+                tt(o, cand(k), Bt("mx%d" % ((k - 2) % 4)), AL.max)
+        for j in range(na):
+            act(piece(2 + j), cand(n2 + j), AF.Copy)
+        if t == 0 or na != NA[t - 1]:
+            iota(R("RS", 0, 256 * np_), [[0, 256], [256, np_]])
+            aff(sf("top"), sf("lane"), float(np_), float(1536 + np_ - 1))
+            if IDS:
+                aff(Ft("idb", 256, 272), sf("top"), 1.0, float(16 * 4096))
+        scan(R("VE", 1536, 1536 + 256 * np_), R("RS", 0, 256 * np_), R("PC", 0, 256 * np_), 0.0, AL.min, AL.max)
+        if IDS:
+            tt(sf("cm"), sf("top"), cur(t), AL.subtract)
         if t == 0:
             codes()
-            pre(0)
-            constants_2()
-            spawn_block(0)
-            cp(su("Lx"), sf("c1"))
         if t == 1:
             to_list(P(6, 0, 128), "id", R("PT", 0, 2048))
-            constants_6()
-        if t == 2:
-            constants_5()
-        parts = [Bt("xa", 256 * j, 256 * j + 256) for j in range(na)] + [Bt("mx%d" % ((n2 - 2) % 4)), Bt("mx%d" % ((n2 - 1) % 4))]
-        total = [parts[0]]
-        for j, x in enumerate(parts[1:]):
-            mm([(P(7, 0, 256), sq("eye"), x)] + [(P(7, 0, 256), sq("neye"), u) for u in total])
-            act(Bt("mr%d" % j), P(7, 0, 256), AF.Relu)
-            total.append(Bt("mr%d" % j))
-        mm([(P(7, 0, 256), sq("eye"), u) for u in total])
-        top = R("VE", 1536, 1792)
-        act(Bt("mt0") if NTAIL else top, P(7, 0, 256), AF.Copy)
-        for j in range(NTAIL):
-            tt(top if j == NTAIL - 1 else Bt("mt%d" % ((j + 1) % 2)), cand(n2 + j), Bt("mt%d" % (j % 2)), AL.max)
         tt(Jt("v", 0, 256), P(0, 0, 256), Ft("cb", 0, 256), AL.subtract)
         ts(Jt("tb"), IX(Jt("v"), su("Lp", 0, 17)), 11, AL.arith_shift_right, 0x1001 | (1 << 20), AL.bitwise_and)
         ts(Jt("nn"), Jt("tb"), 1.0 / 4096, AL.mult, 0.5 - 1.0 / 8192, AL.add)
         ts(Ft("nh"), Jt("nn"), 1.0, AL.not_equal)
-        scan(Ft("sc"), Ft("nh"), Ft("code"), 4194304.0, AL.mult, AL.max)
-        cp(si("s"), Ft("sc", 16, 272, 17))
-        ts(si("al"), si("s"), 4095, AL.bitwise_and)
-        cp(su("al"), si("al"))
-        act(Bt("gf"), IX(R("PT"), su("al")), AF.Copy)
-        to_list(P(1, 0, 16), "id", Bt("gf"))
-        act(Bt("xf"), IX(R("XE"), su("al")), AF.Copy)
-        ts(sf("nr"), si("al"), 2048.0, AL.is_ge)
-        tt(sf("tq"), sf("nr"), sf("cm"), AL.mult)
+        scan(Ft("sc", 0, 272, k=2), Ft("nh"), Ft("code"), 0.0, AL.mult, AL.max)
+        if IDS:
+            act(Ft("idb", 0, 256), P(1, 0, 256), AF.Copy)
+            act(Ft("idt"), IX(Ft("idb"), su("Lp", 0, 17)), AF.Copy)
+            scan(Ft("sc", 272, 544), Ft("nh"), Ft("idt"), 0.0, AL.mult, AL.max)
+            cp(si("s", k=2), Ft("sc", 16, 544, 17))
+            ts(si("al", k=2), si("s"), 4095, AL.bitwise_and)
+            cp(su("al", k=2), si("al"))
+        else:
+            cp(si("s", 0, 16, k=2), Ft("sc", 16, 272, 17))
+            ts(si("al", 0, 16, k=2), si("s", 0, 16), 4095, AL.bitwise_and)
+            cp(su("al", 0, 16, k=2), si("al", 0, 16))
+            act(Bt("gf"), IX(R("PT"), su("al", 0, 16)), AF.Copy)
+            if SHORT and t > 0:
+                idl = to_list_short("idl", 1, "bdq", Bt("gf"))
+            else:
+                to_list(P(1, 0, 16), "id", Bt("gf"))
+                idl = P(1, 0, 16)
+        act(Bt("xf"), IX(R("XE"), su("al", 0, 16)), AF.Copy)
+        ts(sf("nr"), si("al", 0, 16), 2048.0, AL.is_ge)
+        tt(sf("tq"), sf("nr"), sf("cm" if IDS else "top"), AL.mult)
+        if IDS:
+            tt(sf("pc"), si("al", 16, 32), sf("tq"), AL.subtract)
+        else:
+            tt(sf("sl"), idl, sf("tq"), AL.max)
+            cp(su("al", 16, 32), sf("sl"))
+        if PEDF:
+            if PEDF == 1:
+                cp(Bt("vf"), IX(R("VE", 0, 1536 + 256 * np_), su("al", 16, 32)))
+            else:
+                act(Bt("vf"), IX(R("VE", 0, 1536 + 256 * np_), su("al", 16, 32)), AF.Copy)
+            mm([(P(7, 0, 256), sq("neye"), Bt("xf"))], last=False)
+            mm([(P(7, 0, 256), sq("eye"), Bt("vf"))], first=False)
+        else:
+            tt(Bt("df"), IX(R("VE", 0, 1536 + 256 * np_), su("al", 16, 32)), Bt("xf"), AL.subtract)
 
         def same_strand(xs):
             for x in xs:
-                w = 240 - 16 * x
-                o = R("EQ", 256 * (x + 1), 256 * (x + 1) + w)
-                ts(o, su("curR", 256 - w, 256, k=16), sf("key", x, x + 1), AL.is_equal)
-                mm([(P(0, 256 - w, 256), sq("bd"), o)], first=False, last=(x == 14))
+                a = 256 * x
+                ts(R("EQ", a, a + 256 - 16 * x), su("curR", 16 * x, 256, k=16), sf("key", x, x + 1), AL.is_equal)
+                mm([(P(0, 16 * x, 16 * x + 16), sq("bdw"), R("EQ", a, a + 16))]
+                   + ([(P(0, 16 * x + 16, 256), sq("bd"), R("EQ", a + 16, a + 256 - 16 * x))] if x < 15 else []), first=False, last=(x == 15))
 
         if t > 0:
-            ts(sf("pm5"), si("al"), 2048.0, AL.is_ge, 0.5, AL.subtract)
+            ts(sf("pm5"), si("al", 0, 16), 2048.0, AL.is_ge, 0.5, AL.subtract)
             tt(sf("key"), sf("pm5"), sf("c2"), AL.mult)
-            tt(R("EQ", 0, 256), IX(sf("key"), su("Lx")), Ft("curM", 0, 256), AL.is_equal)
-            mm([(P(0, 0, 256), sq("eye"), Bt("nm")), (P(0, 0, 256), sq("bd"), R("EQ", 0, 256))], last=False)
+            ts(sf("nrt"), si("al", 0, 16), 2048.0, AL.is_ge, cf("thr"), AL.mult)
+            mm([(P(0, 0, 256), sq("eye"), Bt("nm"))], last=False)
             same_strand(range(0, 2))
         if t == 1:
             cp(su("Wl"), P(6, 0, 128))
-        tt(sf("sl"), P(1, 0, 16), sf("tq"), AL.add)
-        cp(su("sl"), sf("sl"))
-        tt(Bt("df"), IX(R("VE"), su("sl")), Bt("xf"), AL.subtract)
         yn = R(land, 0, 256)
-        act(yn, Bt("df"), AF.Abs)
+        act(yn, P(7, 0, 256) if PEDF else Bt("df"), AF.Abs)
         trs = []
         for (d, sl_, engs) in first_hop(rank):
             rid, pid = topo.addr(d, core)
@@ -634,16 +806,26 @@ def rank_program(g, core, T, topo):
                                          src=yn[0], dst=T[land][:, 256 * sl_:256 * sl_ + 256]))
             cnt["sent"] = cnt.get("sent", 0) + len(engs)
         emit("g", lambda trs=trs: g.remote_dma_fused(trs, local_sem=sem["sent"]), [R(land, 256, 2048)], [yn],
-             kind="arr%d" % t, time=0.5, late=T_EXCH)
+             kind="arr%d" % t, time=0.5, late=T_EXCH[t])
+        made = len(nodes) - 2
+        left = made if GATE else 0
+        if t == 0:
+            gate.append(made)
+            late_fills()
+            gate.pop()
+            gate.append(left)
+            pre(0)
+            constants_2()
+            spawn_block(0)
+            gate.pop()
         act(Bt("gs"), yn, AF.Sign, bias=col("nth", t))
         if t > 0:
-            same_strand(range(2, 15))
+            same_strand(range(2, 16))
         to_list(P(3, 0, 16), "one", Bt("gs"))
         to_list(P(2, 0, 16), "mark", yn)
         if t > 0:
             scan(Ft("sc", 0, 256), Bt("rst"), P(0, 0, 256), 0.0, AL.add, AL.min)
-            ts(sf("l0"), Ft("sc", 15, 256, 16), 0.0, AL.is_equal)
-            tt(sf("lead"), sf("l0"), sf("nr"), AL.mult)
+            tt(sf("lead"), Ft("sc", 15, 256, 16), sf("nrt"), AL.is_lt)
             lead = sf("lead")
         else:
             lead = sf("nr")
@@ -654,7 +836,7 @@ def rank_program(g, core, T, topo):
         tt(sf("a1"), sp(t), sf("dn"), AL.mult)
         nxt = cur(t + 1) if t < 2 else sf("last")
         tt(sf("vo"), sf("u4"), sf("a1"), AL.add)
-        tt(nxt, P(1, 0, 16), sf("a1"), AL.add)
+        tt(nxt, sf("pc") if IDS else idl, sf("a1"), AL.add)
         cp(su("vo"), sf("vo"))
         cp(su("nc"), nxt)
         cp(IX(R("VE", 0, 1536), su("vo")), yn)
@@ -665,7 +847,11 @@ def rank_program(g, core, T, topo):
             ts(su("zl"), sf("zz"), 16.0, AL.mult)
 
         def cells_of_arrivals(base):
-            cp(si("mz"), P(2, 0, 16))
+            if SHORT:
+                cp(si("mz"), to_list_short("mzl", 2, "bdm", Bt("z")))
+            else:
+                to_list(P(2, 0, 16), "mark", Bt("z"))
+                cp(si("mz"), P(2, 0, 16))
             ts(si("m7"), si("mz"), 7, AL.bitwise_and)
             tt(sf("bo"), si("m7"), sf(base), AL.add)
             cp(su("bo"), sf("bo"))
@@ -674,7 +860,9 @@ def rank_program(g, core, T, topo):
             nv = 768 + 256 * t
             aff(Bt("rb", 0, 16), sf("nr"), -1.0, 1.0)
             mm([(P(7, 0, 16), sq("bd"), Bt("rb", 0, 16))])
-            act(R("XE", 2048, 2304), yn, AF.Copy)
+            gate.append(len(nodes) - 3)
+            move(R("XE", 2048, 2304), yn)
+            gate.pop()
             act(sf("tmp"), P(7, 0, 16), AF.Identity, acc=cf("A"))
             act(LP, IX(R("SP", 0, nv), su("nc")), AF.Copy)
             for c in range(NDV):
@@ -691,28 +879,46 @@ def rank_program(g, core, T, topo):
             codes()
             for c in range(NDV, 4):
                 count(c, True)
+            gate.append(left)
             if t == 0:
                 constants_3()
                 constants_4()
-            inverse(t)
+                constants_6()
+            else:
+                constants_5()
+            for i in INV[t]:
+                inverse(i)
+            gate.pop()
             mm([(P(0, 0, 256), sq("bdid"), LP)])
             cp(su("curR", k=16), P(0, 0, 256))
             act(Bt("z"), IX(R(land), su("zl")), AF.Copy)
-            tt(Bt("g2"), IX(R(land), su("zl")), Bt("vc"), AL.is_lt)
-            to_list(P(2, 0, 16), "mark", Bt("z"))
-            mm([(P(6, 0, 256), sq("dg"), LP), (P(6, 0, 256), Mt("one", 9, 137), Bt("g2"))])
-            act(Bt("lpb"), P(6, 0, 256), AF.Relu, bias=cf("rb"), scale=cf("rs"))
+            if G2A:
+                mm([(P(7, 0, 256), sq("neye"), Bt("vc"))], last=False)
+                mm([(P(7, 0, 256), sq("eye"), Bt("z"))], first=False)
+                act(Bt("g2"), P(7, 0, 256), AF.Sign, bias=0.5)
+            else:
+                tt(Bt("g2"), IX(R(land), su("zl")), Bt("vc"), AL.is_ge)
+            mm([(P(6, 0, 256), sq("dg"), LP)], last=False)
+            mm([(P(6, 0, 256), Mt("one", 9, 137), Bt("g2"))], first=False)
+            act(Bt("lpb"), P(6, 0, 256), AF.Relu, bias=cf("rb2" if G2A else "rb"))
             pre(t + 1)
             cells_of_arrivals("l8")
             cp(IX(R("PT", 0, 2048), su("bo")), Bt("lpb"))
             cp(IX(R("XE", 0, 2048), su("bo")), Bt("z"))
             lane_keys()
-            mm([(P(1, 0, 256), sq("bdid"), LP), (P(1, 0, 256), sq("eye"), Bt("nt"))])
-            act(Ft("curM", 0, 256), P(1, 0, 256), AF.Copy)
             spawn_block(t + 1)
         else:
             act(LP, IX(R("SP"), su("nc")), AF.Copy)
-            store("s", T.yv[:], R("VE", 0, 1280))
+            store("s", T.yv[:], R("VE", 0, 1280), 8, 2560)
+            if WROW:
+                for c in range(4):
+                    mm([(P(4 + c, 0, 512), sq("bdq"), R("PT", 512 * c, 512 * c + 512))])
+                gate.append(made)
+                for c in range(4):
+                    act(R("WF", 512 * c, 512 * c + 512), P(4 + c, 0, 512), AF.Copy)
+                gate.pop()
+                mm([(P(6, 0, 256), sq("bdq"), LP)])
+                act(Ft("wo", 0, 256), P(6, 0, 256), AF.Copy)
             tt(sf("T4"), sf("T4"), sf("sp"), AL.mult)
             cp(si("m"), P(2, 0, 16))
             tt(sf("T4"), sf("T4"), sf("D4"), AL.add)
@@ -720,36 +926,41 @@ def rank_program(g, core, T, topo):
             cp(su("l4", k=4), sf("T4"))
             zlist()
             l0, l1, l2, z0 = [su("l4", 16 * i, 16 * i + 16) for i in range(4)]
-            cp(IX(R("S2"), l2), Bt("two"))
-            act(Bt("g1"), IX(R("S2"), l1), AF.Copy)
-            cp(R("S1", 768, 1536), R("S2", 768, 1536))
+            act(IX(R("S2", 0, 1792), l2), Ft("two", 0, 256), AF.Silu)
+            act(Ft("g1", 0, 256), IX(R("S2", 0, 1536), l1), AF.Copy)
             act(Bt("z"), IX(R(land), su("zl")), AF.Copy)
-            to_list(P(2, 0, 16), "mark", Bt("z"))
-            tt(IX(R("S1"), l1), Bt("g1"), R("S2", 1536, 1792), AL.add)
-            aff(Ft("q1", 0, 256), Bt("g1"), cf("sg"))
-            act(Ft("q0", 0, 256), IX(R("S1"), l0), AF.Identity, scale=cf("sg"))
-            act(R("S0", 256, 512), R("S1", 1024, 1280), AF.Copy)
-            tt(R("S0", 0, 256), IX(R("S1", 1280, 1552), z0), R("S1", 768, 1024), AL.add)
+            tt(IX(R("S2", 0, 1536), l1), Ft("g1", 0, 256), R("S2", 1536, 1792), AL.add)
+            aff(Bt("q1"), Ft("g1", 0, 256), cf("sg64"))
+            act(Bt("q0"), IX(R("S2", 0, 1536), l0), AF.Identity, scale=cf("sg64"))
+            act(R("S0", 256, 512), R("S2", 1024, 1280), AF.Copy)
+            tt(R("S0", 0, 256), IX(R("S2", 1280, 1808), z0), R("S2", 768, 1024), AL.add)
             for i in range(2):
-                act(R("SE", 512 * i, 512 * i + 512), IX(R("S0"), su("inv", 32 * i, 32 * i + 32)), AF.Copy)
+                act(R("SE", 512 * i, 512 * i + 512), IX(R("S0"), su("inv", 32 * i, 32 * i + 32)), AF.Identity, scale=col("oh64", i))
             cells_of_arrivals("l8b")
-            for h in range(2):
-                cp(IX(R("XE", 1024 * h, 1024 * h + 1024), su("bo", 8 * h, 8 * h + 8)), Bt("z", 128 * h, 128 * h + 128))
-                store("s", T.yx[:, 1024 * h:1024 * h + 1024], R("XE", 1024 * h, 1024 * h + 1024))
-            scan(R("CE", 1, 513), R("SE", 0, 512), R("MK", 0, 512), 0.0, AL.add, AL.mult)
-            act(R("RA"), IX(R("CE", 0, 513), su("eh", 0, 32)), AF.Copy)
-            for h in range(2):
-                cp(IX(R("PT", 1024 * h, 1024 * h + 1024), su("bo", 8 * h, 8 * h + 8)), R("PT", 2048 + 128 * h, 2176 + 128 * h))
-                mm([(P(6, 0, 128), Mt("id", 15 - y, 143 - y), R("PT", 128 * y, 128 * y + 128)) for y in range(8 * h, 8 * h + 8)],
-                   first=(h == 0), last=(h == 1))
-            act(Ft("wo", 0, 128), P(6, 0, 128), AF.Copy)
-            store("a", T.yw[:], Ft("wo", 0, 128))
-            scan(R("CE", 528, 1040), R("SE", 512, 1024), R("MK", 512, 1024), -1.0, AL.add, AL.mult)
+            cuts = ((0, CUT), (CUT, 16))
+            for (a, b) in cuts:
+                cp(IX(R("XE", 128 * a, 128 * b), su("bo", a, b)), Bt("z", 16 * a, 16 * b))
+                store("s", T.yx[:, 128 * a:128 * b], R("XE", 128 * a, 128 * b), 8, 6000 if a == 0 else 4400)
+                gate[:] = [len(nodes) - 2] if a == 0 else []
+            scan(R("CE", 1, 513), R("MK"), R("SE", 0, 512), 0.0, AL.mult, AL.add)
+            act(R("RA"), IX(R("CE", 0, 513), su("eh", 0, 32)), AF.Identity, bias=col("oh", 0))
+            if WROW:
+                for (a, b) in cuts:
+                    cp(IX(R("WF", 128 * a, 128 * b), su("bo", a, b)), Ft("wo", 16 * a, 16 * b))
+                store("a", T.yw[:], R("WF", p=(0, 128, 16)), 1, 4096)
+            else:
+                for (a, b) in cuts[::-1]:
+                    cp(IX(R("PT", 128 * a, 128 * b), su("bo", a, b)), R("PT", 2048 + 16 * a, 2048 + 16 * b))
+                    mm([(P(6, 0, 128), Mt("id", 15 - y, 143 - y), R("PT", 128 * y, 128 * y + 128)) for y in range(a, b)],
+                       first=(a > 0), last=(a == 0))
+                act(Ft("wo", 0, 128), P(6, 0, 128), AF.Copy)
+                store("a", T.yw[:], Ft("wo", 0, 128), 8, 512)
+            scan(R("CE", 528, 1040), R("MK"), R("SE", 512, 1024), -1.0, AL.mult, AL.add)
             tt(R("RR", 768, 1280), IX(R("CE", 528, 1040), su("eh", 32, 64)), R("RA"), AL.add)
-            tt(R("RR", 1280, 1536), IX(R("RR", 0, 1280), l0), Ft("q0", 0, 256), AL.add)
-            tt(R("RR", 1536, 1792), IX(R("RR", 0, 1536), l1), Ft("q1", 0, 256), AL.add)
-            ts(R("RR", 1792, 2048), IX(R("RR", 0, 1792), l2), cf("sg"), AL.add)
-            store("s", T.ye[:], R("RR", 768, 2048, p=(0, 128, 16)))
-            store("a", T.yh[:], R("RR", 768, 2048, p=(1, 128, 16)))
+            tt(R("RR", 1280, 1536), IX(R("RR", 0, 1280), l0), Bt("q0"), AL.add)
+            tt(R("RR", 1536, 1792), IX(R("RR", 0, 1536), l1), Bt("q1"), AL.add)
+            act(R("RR", 1792, 2048), IX(R("RR", 0, 1792), l2), AF.Identity, bias=cf("sg"))
+            store("s", T.ye[:], R("RR", 768, 2048, p=(0, 128, 16)), 1, 2560)
+            store("a", T.yh[:], R("RR", 768, 2048, p=(1, 128, 16)), 1, 2560)
 
     issue()

@@ -4,20 +4,17 @@ from concourse.mybir import AluOpType, ActivationFunctionType
 AL = AluOpType
 AF = ActivationFunctionType
 NR = 3
-NDV = 2
+NDV = 3
+NA = [5, 5, 5]
+NP = [3, 2, 2]
+CUT = 4
 T_CALL, T_INDIRECT, T_WAKE, T_LOOK, T_PE, C_PE, T_DMA = 0.015, 0.055, 0.05, 0.5, 0.58, 4, 1.9
 T_ROW, T_BYTE = 0.02, 0.00005
 T_EXCH = [9.5, 7.0, 7.0]
-GATE = False
 PACES = [(0.00097, 1.56, 3.8, 0.05, 0.85, 1.0, 1.0), (0.00087, 1.3, 2.5, 0.1, 1.3, 1.2, 1.1), (0.0012, 1.9, 5.0, 0.06, 1.1, 0.9, 1.2),
          (0.001, 1.3, 5.0, 0.03, 0.75, 1.2, 0.9)]
-PASSES, SWAPS, SHAKE, SEED, HEAT = 15, 32000, 0.5, 3, 0.012
-NA = [4, 4, 4]
-NP = [1, 1, 1]
-NCV = 0
-CUT = 4
-IDS, PEDF, SILU, G2A, SHORT, WROW = False, 0, [1], False, False, False
-INV = [[0, 1], []]
+PASSES, SWAPS, SHAKE, SEED, HEAT = 10, 80000, 0.5, 2, 0.015
+PLACE = [0, 16, 48, 32]
 ORDER = {}
 
 SCRATCH = {
@@ -47,7 +44,7 @@ SCRATCH = {
     "EA": ("sbuf", [128, 128], "bfloat16"),
     "ZS": ("sbuf", [128, 512], "bfloat16"),
     "Z0": ("sbuf", [128, 144], "float32"),
-    "WF": ("sbuf", [128, 2048], "float32"),
+    "WF": ("sbuf", [128, 1280], "float32"),
     "S2": ("sbuf", [128, 1808], "float32"),
     "S0": ("sbuf", [128, 512], "bfloat16"),
     "SE": ("sbuf", [128, 1024], "bfloat16"),
@@ -69,7 +66,9 @@ def routes(T, topo):
     for r, c in enumerate(cores):
         order = [(r + d) % n for d in range(1, n)]
         near = [q for q in order if topo.may_write(c, cores[q])]
-        far = [q for q in order if q not in near]
+        far = sorted(q for q in order if q not in near)
+        j = sorted(near + [r]).index(r)
+        far = far[j:] + far[:j]
         able = [h for h in topo.cores_of(c) if h != c and T.rank_of(h) is None and all(topo.may_write(h, cores[q]) for q in order)]
         turn = far + near
         out.append([(h, turn[i::len(able)]) for i, h in enumerate(able)])
@@ -226,22 +225,33 @@ def rank_program(g, core, T, topo):
         paces = [([nd["cost"][0] + c * (nd["cost"][1] * (pe if nd["e"] == "t" else 1.0) + ga * nd["cost"][2] + sc * nd["cost"][3]) for nd in nodes],
                   [nd["late"] * (ex if nd["kind"][:3] == "arr" else dm) for nd in nodes], wk) for (c, ga, sc, wk, ex, pe, dm) in PACES]
 
-        def replay(seq, pace):
+        waits = [[d for d in pars[i] if not (eng[d] == "t" and eng[i] == "t")] for i in range(m)]
+
+        def replay(seq, pace, old=None, a=0):
             time, late, wake = pace
             free = {e: (0.0, -1) for e in names}
-            end, start, why = [0.0] * m, [0.0] * m, [-1] * m
-            for i in seq:
-                t0, why[i] = free[eng[i]]
-                for d in pars[i]:
-                    if end[d] + wake > t0 and not (eng[d] == "t" and eng[i] == "t"):
-                        t0, why[i] = end[d] + wake, d
-                start[i] = t0
+            if old is None:
+                end, start, why = [0.0] * m, [0.0] * m, [-1] * m
+            else:
+                start, why, end = list(old[1]), list(old[2]), list(old[3])
+                for i in seq[:a]:
+                    free[eng[i]] = (start[i] + time[i], i)
+            for i in seq[a:]:
+                t0, w = free[eng[i]]
+                for d in waits[i]:
+                    if end[d] + wake > t0:
+                        t0, w = end[d] + wake, d
+                start[i], why[i] = t0, w
                 free[eng[i]] = (t0 + time[i], i)
                 end[i] = t0 + time[i] + late[i]
             return max(end), start, why, end
 
         def score(seq):
             return sum(replay(seq, p)[0] / w for p, w in zip(paces, norm))
+
+        def rescore(new, a, runs):
+            runs = [replay(new, p, r, a) for p, r in zip(paces, runs)]
+            return sum(r[0] / w for r, w in zip(runs, norm)), runs
 
         if m not in ORDER:
             best = None
@@ -265,11 +275,12 @@ def rank_program(g, core, T, topo):
                 prio = plan(kids, pars, end, True)[1]
             val, seq = best[0], best[1]
             kept = (val, seq)
+            runs = [replay(seq, p) for p in paces]
             for step in range(SWAPS):
                 if val < kept[0]:
                     kept = (val, seq)
                 slack = 1e-9 + HEAT * (1 - step / SWAPS) ** 2 * draw() * draw()
-                span, start, why, end = replay(seq, paces[int(draw() * len(paces))])
+                span, start, why, end = runs[int(draw() * len(paces))]
                 seq = sorted(seq, key=lambda i: start[i])
                 chain = []
                 i = end.index(span)
@@ -291,9 +302,9 @@ def rank_program(g, core, T, topo):
                         continue
                     a += int(draw() * (b - a))
                     new = seq[:a] + [j] + seq[a:b] + seq[b + 1:]
-                    v = score(new)
+                    v, tried = rescore(new, a, runs)
                     if v <= val + slack:
-                        val, seq = v, new
+                        val, seq, runs = v, new, tried
                     continue
                 a, b = seq.index(j), seq.index(i)
                 early, rest_, moved = [], [], {j}
@@ -311,9 +322,9 @@ def rank_program(g, core, T, topo):
                         break
                     tail.append(k)
                 new = seq[:a] + early + tail + [j] + rest_ + seq[b + 1 + len(tail):]
-                v = score(new)
+                v, tried = rescore(new, a, runs)
                 if v <= val + slack:
-                    val, seq = v, new
+                    val, seq, runs = v, new, tried
             val, seq = min(kept, (val, seq))
             ORDER[m] = (val, seq, [replay(seq, p)[0] for p in paces])
         tok = [None] * m
@@ -391,6 +402,9 @@ def rank_program(g, core, T, topo):
         emit("g", lambda: g.iota(out[0], pat, base, cm, allow_small_or_imprecise_dtypes=True), [out], [],
              time=0.15, cycles=2 * out[3])
 
+    def select(x, pat, op, c, base, cm):
+        emit("g", lambda: g.affine_select(x[0], x[0], pat, op, c, base, cm), [x], [x], time=0.2, cycles=2 * x[3])
+
     def memset(out, c):
         emit("v", lambda: g.vector.memset(out[0], c), [out], [], rate=0.5)
 
@@ -429,12 +443,6 @@ def rank_program(g, core, T, topo):
         nm, a, b = src[1][0]
         mm([(out, Mt(z, 15 - y, 143 - y), R(nm, a + y, b, 16)) for y in range(16)])
 
-    def to_list_short(name, bank, block, src):
-        mm([(P(bank, 0, 256), sq("eye"), Bt("nm"))], last=False)
-        mm([(P(bank, 0, 256), sq(block), src)], first=False)
-        scan(Ft(name, 0, 256), Bt("rst"), P(bank, 0, 256), 0.0, AL.add, AL.min)
-        return Ft(name, 15, 256, 16)
-
     def col(name, i):
         return cf(name, i, i + 1)
 
@@ -472,12 +480,12 @@ def rank_program(g, core, T, topo):
     fill(R("VE", 512, 1536), 0)
 
     def late_fills():
-        iota(Ft("y", 0, 256), [[0, 16], [1, 16]])
+        iota(sf("d4", k=2), [[-256, 2], [16, 16]], 512)
         fill(R("S2", 0, 1792), 64)
         fill(R("S2", 1792, 1808), 0)
         fill(Ft("two", 0, 256), 128)
         fill(R("CE", 0, 8), 0)
-        fill(sf("D4", 48, 64, k=4), 512)
+        fill(sf("D4", 32, 48, k=4), 512)
 
     ts(si("p", 1, 2), si("p", 0, 1), 15, AL.bitwise_and)
     ts(si("p", 2, 3), si("p", 0, 1), 4, AL.arith_shift_right)
@@ -506,8 +514,6 @@ def rank_program(g, core, T, topo):
     aff(cf("rb"), col("oh", 6), -5.0)
     aff(Mt("d5"), Mt("eye"), col("oh", 5))
     aff(cf("bias1"), col("oh", 4), 256.0, cf("bias0"))
-    if IDS:
-        aff(Bt("prio"), Ft("k", 0, 256), 4096.0)
     aff(Mt("dg"), Mt("eye"), cf("pass"))
     onehot(cf("q", k=8), sf("tmp", 0, 8), sf("c1", 0, 8), col("nb", 6))
     act(Mt("one"), Mt("mark"), AF.Sign)
@@ -527,8 +533,9 @@ def rank_program(g, core, T, topo):
         tt(si("sq"), si("u"), si("u"), AL.mult)
         tt(Ft("t1", 0, 256), IX(si("u"), su("Lb")), Ft("kap", 0, 256), AL.mult)
         ts(si("sh"), si("sq"), 5, AL.arith_shift_right)
-        ts(sf("base"), si("sh"), cf("A") if t > 0 else 0.0, AL.add)
-        tt(Jt("s", 0, 256), IX(sf("base"), su("Lb")), Ft("t1", 0, 256), AL.add)
+        if t > 0:
+            ts(sf("base"), si("sh"), cf("A"), AL.add)
+        tt(Jt("s", 0, 256), IX(sf("base") if t > 0 else si("sh"), su("Lb")), Ft("t1", 0, 256), AL.add)
         ts(Jt("a", 0, 256), Jt("s", 0, 256), 2047, AL.bitwise_and)
         cp(su("tile", k=16), Jt("a", 0, 256))
 
@@ -566,13 +573,10 @@ def rank_program(g, core, T, topo):
         a, b, l = blk(c)
         act(R("GT", a, b), P(6 + c % 2, 0, 512), AF.Sign, bias=0.5)
 
-    def count(c, signs, vec=False):
+    def count(c, signs):
         a, b, l = blk(c)
         mm([(P(4 + c % 2, 0, 512), sq("dg"), R("PT", a, b)), (P(4 + c % 2, 0, 512), Mt("one", 9, 137), R("GT", a, b))])
-        if vec:
-            ts(R("PT", a, b), P(4 + c % 2, 0, 512), cf("rb"), AL.add, 0.0, AL.max)
-        else:
-            act(R("PT", a, b), P(4 + c % 2, 0, 512), AF.Relu, bias=cf("rb2" if signs else "rb"))
+        act(R("PT", a, b), P(4 + c % 2, 0, 512), AF.Relu, bias=cf("rb2" if signs else "rb"))
 
     def lane_keys():
         to_list(P(3, 0, 16), "key", LP)
@@ -581,7 +585,7 @@ def rank_program(g, core, T, topo):
 
     for c in range(4):
         greater_v(c, 512)
-        count(c, False, c >= 4 - NCV)
+        count(c, False)
     tile(0)
     lane_keys()
 
@@ -589,14 +593,14 @@ def rank_program(g, core, T, topo):
         return sf("cur", 16 * t, 16 * t + 16, k=3)
 
     def sp(t):
-        return sf("sp", 16 * t, 16 * t + 16, k=4)
+        return sf("sp", PLACE[t], PLACE[t] + 16, k=4)
 
     def pre(t):
         tt(sf("cdm"), cur(t), sf("dum"), AL.subtract)
         aff(sf("dn"), sf("cdm"), -1.0, float(512 + 256 * t - 1280))
-        aff(sf("T4", 16 * t, 16 * t + 16, k=4), sf("cdm"), 1.0, float(768 + 1280 - 512 + 256 * t))
+        aff(sf("T4", PLACE[t], PLACE[t] + 16, k=4), sf("cdm"), 1.0, float(768 + 1280 - 512 + 256 * t))
         if t > 0:
-            aff(sf("c2"), cur(t), 2.0, 2.0)
+            aff(sf("c2"), cur(t), 1.0, 1.0)
 
     def spawn_block(t):
         o = P(5, 0, 256)
@@ -624,7 +628,9 @@ def rank_program(g, core, T, topo):
         aff(cf("b4", k=3), cf("b3"), col("oh", 4))
         for t in range(2):
             aff(cf("bs", t, t + 1, k=2), cf("dl"), 0.5 ** (t + 1), col("b4", t))
-        onehot(sq("bd"), Ft("tmp", 0, 128), Ft("k", 0, 128), col("nb", 2))
+        fill(sq("bd"), 1)
+        select(sq("bd"), [[-16, 8], [0, 16]], AL.is_ge, 0.0, 0, 1)
+        select(sq("bd"), [[16, 8], [0, 16]], AL.is_ge, 0.0, 15, -1)
         aff(sf("l16"), sf("lane"), 1.0 / 16)
         aff(sf("l8"), sf("lane"), 8.0)
         aff(cf("rb2"), col("oh", 6), 5.0)
@@ -634,19 +640,18 @@ def rank_program(g, core, T, topo):
         scan(sf("pw"), sf("hf"), sf("hf"), 1.0, AL.mult, AL.mult)
         tt(sf("hf"), sf("pw"), cf("oh"), AL.mult)
         act(sf("pw"), sf("hf"), AF.Identity, acc=cf("w4"))
-        aff(cf("t9"), pm, -65536.0)
-        if SHORT or WROW:
-            aff(sq("bdq"), sq("bd"), col("q", 2))
-        if SHORT:
-            aff(sq("bdm"), sq("bd"), cf("wm"))
         aff(sq("bdw"), sq("bd"), cf("w4"))
         aff(cf("thr"), cf("w4"), 2.0)
         aff(cf("wi1"), col("q", 2), 1.0, col("oh", 8))
         aff(sq("bdid"), sq("bd"), cf("wi1"))
-        act(Bt("nm"), Ft("y", 0, 256), AF.Abs, bias=cf("t9"), scale=65536.0)
+        gate.append(made)
+        fill(Mt("row", 0, 128, p=(0, 16)), 1)
+        select(Mt("row", 0, 128, p=(0, 16)), [[0, 8], [1, 16]], AL.is_equal, 0.0, 0, -1)
+        fill(Bt("nm", p=(0, 16)), 65536)
+        select(Bt("nm", p=(0, 16)), [[0, 16], [1, 16]], AL.not_equal, 0.0, 0, -1)
         fill(Bt("rst"), 0)
-        emit("g", lambda: g.affine_select(Bt("rst")[0], Bt("rst")[0], [[0, 16], [1, 16]], AL.is_gt, 2097152.0, 0, 0),
-             [Bt("rst")], [Bt("rst")], time=0.2, cycles=512)
+        select(Bt("rst"), [[0, 16], [1, 16]], AL.is_gt, 2097152.0, 0, 0)
+        gate.pop()
 
     def constants_4():
         aff(cf("m4"), col("oh", 8), -4.0)
@@ -657,32 +662,27 @@ def rank_program(g, core, T, topo):
         cp(su("eh", k=4), P(1, 0, 64))
 
     def inverse(i):
-        if i not in SILU:
-            for h in range(2):
-                cp(IX(R("SE", 512 * i, 512 * i + 512), su("eh", 32 * i + 16 * h, 32 * i + 16 * h + 16)), R("SP", 256 * h, 256 * h + 256))
-            to_list(P(1, 0, 32), "id", R("SE", 512 * i, 512 * i + 512))
-            cp(su("inv", 32 * i, 32 * i + 32, k=4), P(1, 0, 32))
-            return
-        if i == SILU[0]:
+        if i == 0:
             iota(R("RA"), [[1, 512]], 64)
             aff(R("Z0"), Mt("one"), col("oh", 0))
-        a = 1024 + 512 * i
         for h in range(2):
-            act(IX(R("WF", a, a + 512), su("eh", 32 * i + 16 * h, 32 * i + 16 * h + 16)), R("RA", 256 * h, 256 * h + 256), AF.Silu)
-            if i == SILU[0] and h == 0:
+            act(IX(R("WF", 768, 1280), su("eh", 32 * i + 16 * h, 32 * i + 16 * h + 16)), R("RA", 256 * h, 256 * h + 256), AF.Silu)
+            if i + h == 0:
                 nd = nodes[-1]
                 nd["cost"] = (nd["cost"][0], 1570, 0, nd["cost"][3])
                 nd["time"] += 1.5
-        mm([(P(1, 0, 32), R("Z0", 15 - y, 143 - y), R("WF", a + y, a + 512, 16)) for y in range(16)], wide=4)
+        for h in range(4):
+            mm([(P(1, 0, 32), R("Z0", 15 - y, 143 - y), R("WF", 768 + y, 1280, 16)) for y in range(4 * h, 4 * h + 4)],
+               first=(h == 0), last=(h == 3), wide=4)
         ts(su("inv", 32 * i, 32 * i + 32, k=4), P(1, 0, 32), 64.0, AL.subtract)
 
     def constants_6():
         aff(cf("sg"), col("oh", 1), -1.0, col("oh", 0))
         aff(cf("sg64"), cf("sg"), 1.0 / 64)
         aff(cf("oh64", k=2), cf("oh", 0, 2), 1.0 / 64)
-        for i, o in enumerate((512.0, 256.0, 0.0)):
-            aff(sf("D4", 16 * i, 16 * i + 16), sf("lane"), 1.0, o)
-        aff(sf("T4", 48, 64), sf("lane"), 1.0, -512.0)
+        aff(sf("D4", 0, 32), sf("d4"), 1.0, pm)
+        aff(sf("D4", 48, 64), sf("lane"))
+        aff(sf("T4", 32, 48), sf("lane"), 1.0, -512.0)
         aff(sp(3), sp(0))
         aff(sf("l8b", 0, CUT), sf("l8", 0, CUT))
         aff(sf("l8b", CUT, 16), sf("l8", CUT, 16), 1.0, -128.0 * CUT)
@@ -707,11 +707,7 @@ def rank_program(g, core, T, topo):
             if k0 < k1:
                 act(R("G", 256 * k0, 256 * k1), IX(R("PT", 0, 2048), su("tile", 16 * k0, 16 * k1)), AF.Copy)
         for c in ([1, 0, 2, 3] if NP[t] else range(4)):
-            to_list(P(0, 64 * c, 64 * c + 64), "key", R("G", 1024 * c, 1024 * c + 1024))
-            o = P(1, 64 * c, 64 * c + 64)
-            if IDS:
-              mm([(o, sq("eye"), Bt("prio", 64 * c, 64 * c + 64))]
-               + [(o, Mt("id", 15 - y, 143 - y), R("G", 1024 * c + y, 1024 * c + 1024, 16)) for y in range(16)])
+            to_list(P(1 if c == 3 else 0, 64 * c, 64 * c + 64), "key", R("G", 1024 * c, 1024 * c + 1024))
         na = NA[t]
         n2 = 16 - na
         np_ = na + 2
@@ -733,54 +729,28 @@ def rank_program(g, core, T, topo):
         if t == 0 or na != NA[t - 1]:
             iota(R("RS", 0, 256 * np_), [[0, 256], [256, np_]])
             aff(sf("top"), sf("lane"), float(np_), float(1536 + np_ - 1))
-            if IDS:
-                aff(Ft("idb", 256, 272), sf("top"), 1.0, float(16 * 4096))
         scan(R("VE", 1536, 1536 + 256 * np_), R("RS", 0, 256 * np_), R("PC", 0, 256 * np_), 0.0, AL.min, AL.max)
-        if IDS:
-            tt(sf("cm"), sf("top"), cur(t), AL.subtract)
         if t == 0:
             codes()
         if t == 1:
             to_list(P(6, 0, 128), "id", R("PT", 0, 2048))
-        tt(Jt("v", 0, 256), P(0, 0, 256), Ft("cb", 0, 256), AL.subtract)
+        tt(Jt("v", 0, 192), P(0, 0, 192), Ft("cb", 0, 192), AL.subtract)
+        tt(Jt("v", 192, 256), P(1, 192, 256), Ft("cb", 192, 256), AL.subtract)
         ts(Jt("tb"), IX(Jt("v"), su("Lp", 0, 17)), 11, AL.arith_shift_right, 0x1001 | (1 << 20), AL.bitwise_and)
         ts(Jt("nn"), Jt("tb"), 1.0 / 4096, AL.mult, 0.5 - 1.0 / 8192, AL.add)
         ts(Ft("nh"), Jt("nn"), 1.0, AL.not_equal)
-        scan(Ft("sc", 0, 272, k=2), Ft("nh"), Ft("code"), 0.0, AL.mult, AL.max)
-        if IDS:
-            act(Ft("idb", 0, 256), P(1, 0, 256), AF.Copy)
-            act(Ft("idt"), IX(Ft("idb"), su("Lp", 0, 17)), AF.Copy)
-            scan(Ft("sc", 272, 544), Ft("nh"), Ft("idt"), 0.0, AL.mult, AL.max)
-            cp(si("s", k=2), Ft("sc", 16, 544, 17))
-            ts(si("al", k=2), si("s"), 4095, AL.bitwise_and)
-            cp(su("al", k=2), si("al"))
-        else:
-            cp(si("s", 0, 16, k=2), Ft("sc", 16, 272, 17))
-            ts(si("al", 0, 16, k=2), si("s", 0, 16), 4095, AL.bitwise_and)
-            cp(su("al", 0, 16, k=2), si("al", 0, 16))
-            act(Bt("gf"), IX(R("PT"), su("al", 0, 16)), AF.Copy)
-            if SHORT and t > 0:
-                idl = to_list_short("idl", 1, "bdq", Bt("gf"))
-            else:
-                to_list(P(1, 0, 16), "id", Bt("gf"))
-                idl = P(1, 0, 16)
-        act(Bt("xf"), IX(R("XE"), su("al", 0, 16)), AF.Copy)
-        ts(sf("nr"), si("al", 0, 16), 2048.0, AL.is_ge)
-        tt(sf("tq"), sf("nr"), sf("cm" if IDS else "top"), AL.mult)
-        if IDS:
-            tt(sf("pc"), si("al", 16, 32), sf("tq"), AL.subtract)
-        else:
-            tt(sf("sl"), idl, sf("tq"), AL.max)
-            cp(su("al", 16, 32), sf("sl"))
-        if PEDF:
-            if PEDF == 1:
-                cp(Bt("vf"), IX(R("VE", 0, 1536 + 256 * np_), su("al", 16, 32)))
-            else:
-                act(Bt("vf"), IX(R("VE", 0, 1536 + 256 * np_), su("al", 16, 32)), AF.Copy)
-            mm([(P(7, 0, 256), sq("neye"), Bt("xf"))], last=False)
-            mm([(P(7, 0, 256), sq("eye"), Bt("vf"))], first=False)
-        else:
-            tt(Bt("df"), IX(R("VE", 0, 1536 + 256 * np_), su("al", 16, 32)), Bt("xf"), AL.subtract)
+        scan(Ft("sc"), Ft("nh"), Ft("code"), 0.0, AL.mult, AL.max)
+        cp(si("s"), Ft("sc", 16, 272, 17))
+        ts(si("al"), si("s"), 4095, AL.bitwise_and)
+        cp(su("al"), si("al"))
+        act(Bt("gf"), IX(R("PT"), su("al")), AF.Copy)
+        to_list(P(1, 0, 16), "id", Bt("gf"))
+        act(Bt("xf"), IX(R("XE"), su("al")), AF.Copy)
+        ts(Bt("nr", 0, 16), si("al"), 2048.0, AL.is_ge)
+        tt(sf("tq"), Bt("nr", 0, 16), sf("top"), AL.mult)
+        tt(sf("sl"), P(1, 0, 16), sf("tq"), AL.max)
+        cp(su("sl"), sf("sl"))
+        tt(Bt("df"), IX(R("VE", 0, 1536 + 256 * np_), su("sl")), Bt("xf"), AL.subtract)
 
         def same_strand(xs):
             for x in xs:
@@ -790,15 +760,14 @@ def rank_program(g, core, T, topo):
                    + ([(P(0, 16 * x + 16, 256), sq("bd"), R("EQ", a + 16, a + 256 - 16 * x))] if x < 15 else []), first=False, last=(x == 15))
 
         if t > 0:
-            ts(sf("pm5"), si("al", 0, 16), 2048.0, AL.is_ge, 0.5, AL.subtract)
-            tt(sf("key"), sf("pm5"), sf("c2"), AL.mult)
-            ts(sf("nrt"), si("al", 0, 16), 2048.0, AL.is_ge, cf("thr"), AL.mult)
-            mm([(P(0, 0, 256), sq("eye"), Bt("nm"))], last=False)
+            tt(sf("key"), Bt("nr", 0, 16), sf("c2"), AL.mult)
+            ts(sf("nrt"), si("al"), 2048.0, AL.is_ge, cf("thr"), AL.mult)
+            mm([(P(0, 0, 256), Mt("row", 0, 128, p=(0, 16)), Bt("nm", p=(0, 16)))], last=False)
             same_strand(range(0, 2))
         if t == 1:
             cp(su("Wl"), P(6, 0, 128))
         yn = R(land, 0, 256)
-        act(yn, P(7, 0, 256) if PEDF else Bt("df"), AF.Abs)
+        act(yn, Bt("df"), AF.Abs)
         trs = []
         for (d, sl_, engs) in first_hop(rank):
             rid, pid = topo.addr(d, core)
@@ -808,16 +777,13 @@ def rank_program(g, core, T, topo):
         emit("g", lambda trs=trs: g.remote_dma_fused(trs, local_sem=sem["sent"]), [R(land, 256, 2048)], [yn],
              kind="arr%d" % t, time=0.5, late=T_EXCH[t])
         made = len(nodes) - 2
-        left = made if GATE else 0
         if t == 0:
             gate.append(made)
             late_fills()
             gate.pop()
-            gate.append(left)
             pre(0)
             constants_2()
             spawn_block(0)
-            gate.pop()
         act(Bt("gs"), yn, AF.Sign, bias=col("nth", t))
         if t > 0:
             same_strand(range(2, 16))
@@ -828,7 +794,7 @@ def rank_program(g, core, T, topo):
             tt(sf("lead"), Ft("sc", 15, 256, 16), sf("nrt"), AL.is_lt)
             lead = sf("lead")
         else:
-            lead = sf("nr")
+            lead = Bt("nr", 0, 16)
         tt(sf("u3"), sf("cdm"), lead, AL.mult)
         ts(sf("wl"), P(3, 0, 16), 2.0, AL.is_ge)
         tt(sf("u4"), sf("u3"), sf("dum"), AL.add)
@@ -836,10 +802,11 @@ def rank_program(g, core, T, topo):
         tt(sf("a1"), sp(t), sf("dn"), AL.mult)
         nxt = cur(t + 1) if t < 2 else sf("last")
         tt(sf("vo"), sf("u4"), sf("a1"), AL.add)
-        tt(nxt, sf("pc") if IDS else idl, sf("a1"), AL.add)
+        tt(nxt, P(1, 0, 16), sf("a1"), AL.add)
         cp(su("vo"), sf("vo"))
         cp(su("nc"), nxt)
         cp(IX(R("VE", 0, 1536), su("vo")), yn)
+        written = len(nodes) - 1
 
         def zlist():
             ts(si("d"), si("u"), 0x70, AL.bitwise_and)
@@ -847,23 +814,19 @@ def rank_program(g, core, T, topo):
             ts(su("zl"), sf("zz"), 16.0, AL.mult)
 
         def cells_of_arrivals(base):
-            if SHORT:
-                cp(si("mz"), to_list_short("mzl", 2, "bdm", Bt("z")))
-            else:
-                to_list(P(2, 0, 16), "mark", Bt("z"))
-                cp(si("mz"), P(2, 0, 16))
+            to_list(P(2, 0, 16), "mark", Bt("z"))
+            cp(si("mz"), P(2, 0, 16))
             ts(si("m7"), si("mz"), 7, AL.bitwise_and)
             tt(sf("bo"), si("m7"), sf(base), AL.add)
             cp(su("bo"), sf("bo"))
 
         if t < 2:
             nv = 768 + 256 * t
-            aff(Bt("rb", 0, 16), sf("nr"), -1.0, 1.0)
-            mm([(P(7, 0, 16), sq("bd"), Bt("rb", 0, 16))])
-            gate.append(len(nodes) - 3)
+            mm([(P(7, 0, 16), sq("bd"), Bt("nr", 0, 16))])
+            gate.append(written)
             move(R("XE", 2048, 2304), yn)
             gate.pop()
-            act(sf("tmp"), P(7, 0, 16), AF.Identity, acc=cf("A"))
+            act(sf("tmp"), P(7, 0, 16), AF.Identity, scale=-1.0, bias=16.0, acc=cf("A"))
             act(LP, IX(R("SP", 0, nv), su("nc")), AF.Copy)
             for c in range(NDV):
                 greater_v(c, nv)
@@ -879,28 +842,20 @@ def rank_program(g, core, T, topo):
             codes()
             for c in range(NDV, 4):
                 count(c, True)
-            gate.append(left)
             if t == 0:
                 constants_3()
                 constants_4()
                 constants_6()
             else:
                 constants_5()
-            for i in INV[t]:
-                inverse(i)
-            gate.pop()
+            inverse(t)
             mm([(P(0, 0, 256), sq("bdid"), LP)])
             cp(su("curR", k=16), P(0, 0, 256))
             act(Bt("z"), IX(R(land), su("zl")), AF.Copy)
-            if G2A:
-                mm([(P(7, 0, 256), sq("neye"), Bt("vc"))], last=False)
-                mm([(P(7, 0, 256), sq("eye"), Bt("z"))], first=False)
-                act(Bt("g2"), P(7, 0, 256), AF.Sign, bias=0.5)
-            else:
-                tt(Bt("g2"), IX(R(land), su("zl")), Bt("vc"), AL.is_ge)
+            tt(Bt("g2"), IX(R(land), su("zl")), Bt("vc"), AL.is_ge)
             mm([(P(6, 0, 256), sq("dg"), LP)], last=False)
             mm([(P(6, 0, 256), Mt("one", 9, 137), Bt("g2"))], first=False)
-            act(Bt("lpb"), P(6, 0, 256), AF.Relu, bias=cf("rb2" if G2A else "rb"))
+            act(Bt("lpb"), P(6, 0, 256), AF.Relu, bias=cf("rb"))
             pre(t + 1)
             cells_of_arrivals("l8")
             cp(IX(R("PT", 0, 2048), su("bo")), Bt("lpb"))
@@ -910,22 +865,14 @@ def rank_program(g, core, T, topo):
         else:
             act(LP, IX(R("SP"), su("nc")), AF.Copy)
             store("s", T.yv[:], R("VE", 0, 1280), 8, 2560)
-            if WROW:
-                for c in range(4):
-                    mm([(P(4 + c, 0, 512), sq("bdq"), R("PT", 512 * c, 512 * c + 512))])
-                gate.append(made)
-                for c in range(4):
-                    act(R("WF", 512 * c, 512 * c + 512), P(4 + c, 0, 512), AF.Copy)
-                gate.pop()
-                mm([(P(6, 0, 256), sq("bdq"), LP)])
-                act(Ft("wo", 0, 256), P(6, 0, 256), AF.Copy)
-            tt(sf("T4"), sf("T4"), sf("sp"), AL.mult)
+            for (a, b) in ((0, 48), (48, 64)):
+                tt(sf("T4", a, b), sf("T4", a, b), sf("sp", a, b), AL.mult)
+                tt(sf("T4", a, b), sf("T4", a, b), sf("D4", a, b), AL.add)
+                cp(su("l4", a, b, k=4), sf("T4", a, b))
             cp(si("m"), P(2, 0, 16))
-            tt(sf("T4"), sf("T4"), sf("D4"), AL.add)
             ts(si("u"), si("m"), 4095, AL.bitwise_and)
-            cp(su("l4", k=4), sf("T4"))
             zlist()
-            l0, l1, l2, z0 = [su("l4", 16 * i, 16 * i + 16) for i in range(4)]
+            l0, l1, z0, l2 = [su("l4", 16 * i, 16 * i + 16) for i in range(4)]
             act(IX(R("S2", 0, 1792), l2), Ft("two", 0, 256), AF.Silu)
             act(Ft("g1", 0, 256), IX(R("S2", 0, 1536), l1), AF.Copy)
             act(Bt("z"), IX(R(land), su("zl")), AF.Copy)
@@ -934,8 +881,8 @@ def rank_program(g, core, T, topo):
             act(Bt("q0"), IX(R("S2", 0, 1536), l0), AF.Identity, scale=cf("sg64"))
             act(R("S0", 256, 512), R("S2", 1024, 1280), AF.Copy)
             tt(R("S0", 0, 256), IX(R("S2", 1280, 1808), z0), R("S2", 768, 1024), AL.add)
-            for i in range(2):
-                act(R("SE", 512 * i, 512 * i + 512), IX(R("S0"), su("inv", 32 * i, 32 * i + 32)), AF.Identity, scale=col("oh64", i))
+            act(R("SE", 0, 512), IX(R("S0"), su("inv", 0, 32)), AF.Identity, scale=col("oh64", 0))
+            ts(R("SE", 512, 1024), IX(R("S0"), su("inv", 32, 64)), col("oh64", 1), AL.mult)
             cells_of_arrivals("l8b")
             cuts = ((0, CUT), (CUT, 16))
             for (a, b) in cuts:
@@ -943,20 +890,18 @@ def rank_program(g, core, T, topo):
                 store("s", T.yx[:, 128 * a:128 * b], R("XE", 128 * a, 128 * b), 8, 6000 if a == 0 else 4400)
                 gate[:] = [len(nodes) - 2] if a == 0 else []
             scan(R("CE", 1, 513), R("MK"), R("SE", 0, 512), 0.0, AL.mult, AL.add)
-            act(R("RA"), IX(R("CE", 0, 513), su("eh", 0, 32)), AF.Identity, bias=col("oh", 0))
-            if WROW:
-                for (a, b) in cuts:
-                    cp(IX(R("WF", 128 * a, 128 * b), su("bo", a, b)), Ft("wo", 16 * a, 16 * b))
-                store("a", T.yw[:], R("WF", p=(0, 128, 16)), 1, 4096)
-            else:
-                for (a, b) in cuts[::-1]:
-                    cp(IX(R("PT", 128 * a, 128 * b), su("bo", a, b)), R("PT", 2048 + 16 * a, 2048 + 16 * b))
-                    mm([(P(6, 0, 128), Mt("id", 15 - y, 143 - y), R("PT", 128 * y, 128 * y + 128)) for y in range(a, b)],
-                       first=(a > 0), last=(a == 0))
-                act(Ft("wo", 0, 128), P(6, 0, 128), AF.Copy)
-                store("a", T.yw[:], Ft("wo", 0, 128), 8, 512)
+            for h in range(2):
+                act(R("RA", 256 * h, 256 * h + 256), IX(R("CE", 0, 513), su("eh", 16 * h, 16 * h + 16)), AF.Identity, bias=col("oh", 0))
+            for (a, b) in cuts[::-1]:
+                cp(IX(R("PT", 128 * a, 128 * b), su("bo", a, b)), R("PT", 2048 + 16 * a, 2048 + 16 * b))
+                mm([(P(6, 0, 128), Mt("id", 15 - y, 143 - y), R("PT", 128 * y, 128 * y + 128)) for y in range(a, b)],
+                   first=(a > 0), last=(a == 0))
+            act(Ft("wo", 0, 128), P(6, 0, 128), AF.Copy)
+            store("a", T.yw[:], Ft("wo", 0, 128), 8, 512)
             scan(R("CE", 528, 1040), R("MK"), R("SE", 512, 1024), -1.0, AL.mult, AL.add)
-            tt(R("RR", 768, 1280), IX(R("CE", 528, 1040), su("eh", 32, 64)), R("RA"), AL.add)
+            for h in range(2):
+                tt(R("RR", 768 + 256 * h, 1024 + 256 * h), IX(R("CE", 528, 1040), su("eh", 32 + 16 * h, 48 + 16 * h)),
+                   R("RA", 256 * h, 256 * h + 256), AL.add)
             tt(R("RR", 1280, 1536), IX(R("RR", 0, 1280), l0), Bt("q0"), AL.add)
             tt(R("RR", 1536, 1792), IX(R("RR", 0, 1536), l1), Bt("q1"), AL.add)
             act(R("RR", 1792, 2048), IX(R("RR", 0, 1792), l2), AF.Identity, bias=cf("sg"))

from concourse.bass import DstId, RemoteDMATransfer
from concourse.mybir import AluOpType, ActivationFunctionType

AL = AluOpType
AF = ActivationFunctionType
NR = 3
NDV = 3
NA = [5, 5, 5]
NP = [3, 2, 2]
CUT = 4
T_CALL, T_INDIRECT, T_WAKE, T_LOOK, T_PE, C_PE, T_DMA = 0.015, 0.055, 0.05, 0.5, 0.58, 4, 1.9
T_ROW, T_BYTE = 0.02, 0.00005
T_EXCH = [9.5, 7.0, 7.0]
PACES = [(0.00097, 1.56, 3.8, 0.05, 0.85, 1.0, 1.0), (0.00087, 1.3, 2.5, 0.1, 1.3, 1.2, 1.1), (0.0012, 1.9, 5.0, 0.06, 1.1, 0.9, 1.2),
         (0.001, 1.3, 5.0, 0.03, 0.75, 1.2, 0.9)]
PASSES, SWAPS, SHAKE, SEED, HEAT = 10, 80000, 0.5, 2, 0.015
PLACE = [0, 16, 48, 32]
ORDER = {}

SCRATCH = {
    "XE": ("sbuf", [128, 2304], "bfloat16"),
    "VE": ("sbuf", [128, 3584], "bfloat16"),
    "PC": ("sbuf", [128, 2048], "bfloat16"),
    "RS": ("sbuf", [128, 2048], "bfloat16"),
    "PT": ("sbuf", [128, 2304], "bfloat16"),
    "SP": ("sbuf", [128, 1280], "bfloat16"),
    "G": ("sbuf", [128, 4096], "bfloat16"),
    "GT": ("sbuf", [128, 2048], "bfloat16"),
    "VW": ("sbuf", [128, 2048], "bfloat16"),
    "EQ": ("sbuf", [128, 4096], "bfloat16"),
    "land0": ("sbuf", [128, 2048], "bfloat16"),
    "land1": ("sbuf", [128, 2048], "bfloat16"),
    "land2": ("sbuf", [128, 2048], "bfloat16"),
    "B": ("sbuf", [128, 7680], "bfloat16"),
    "F": ("sbuf", [128, 6528], "float32"),
    "J": ("sbuf", [128, 2448], "int32"),
    "M": ("sbuf", [128, 2880], "bfloat16"),
    "sf": ("sbuf", [128, 1024], "float32"),
    "si": ("sbuf", [128, 320], "int32"),
    "su": ("sbuf", [128, 1152], "uint16"),
    "cf": ("sbuf", [128, 112], "float32"),
    "thb": ("sbuf", [128, 8], "bfloat16"),
    "EH": ("sbuf", [128, 128], "int32"),
    "EA": ("sbuf", [128, 128], "bfloat16"),
    "ZS": ("sbuf", [128, 512], "bfloat16"),
    "Z0": ("sbuf", [128, 144], "float32"),
    "WF": ("sbuf", [128, 1280], "float32"),
    "S2": ("sbuf", [128, 1808], "float32"),
    "S0": ("sbuf", [128, 512], "bfloat16"),
    "SE": ("sbuf", [128, 1024], "bfloat16"),
    "MK": ("sbuf", [128, 512], "bfloat16"),
    "CE": ("sbuf", [128, 1040], "float32"),
    "RA": ("sbuf", [128, 512], "float32"),
    "RR": ("sbuf", [128, 2048], "float32"),
}
for _i in range(8):
    SCRATCH["p%d" % _i] = ("psum", [128, 512], "float32")

SEMAPHORES = ["cv", "ca", "ct", "cg", "sent"] + ["arr%d" % _i for _i in range(NR)] + ["d%d" % _i for _i in range(24)]


def routes(T, topo):
    cores = list(T.cores)
    n = len(cores)
    out = []
    for r, c in enumerate(cores):
        order = [(r + d) % n for d in range(1, n)]
        near = [q for q in order if topo.may_write(c, cores[q])]
        far = sorted(q for q in order if q not in near)
        j = sorted(near + [r]).index(r)
        far = far[j:] + far[:j]
        able = [h for h in topo.cores_of(c) if h != c and T.rank_of(h) is None and all(topo.may_write(h, cores[q]) for q in order)]
        turn = far + near
        out.append([(h, turn[i::len(able)]) for i, h in enumerate(able)])
    return out


def bits(engs):
    m = 0
    for e in engs:
        m |= 1 << e
    return m


def rank_program(g, core, T, topo):
    rank = T.rank_of(core)
    cores = list(T.cores)
    n = len(cores)
    rt = routes(T, topo)
    sem = T.sem

    def slot(t, src, dst):
        d = (src - dst) % n
        return T["land%d" % t][:, 256 * d:256 * d + 256]

    def first_hop(r):
        c = cores[r]
        on = topo.engines(c, rt[r][0][0])
        k = len(on) // len(rt[r])
        return [(h, 0, on[i * k:(i + 1) * k]) for i, (h, _) in enumerate(rt[r])]

    if rank is None:
        for r in range(n):
            for (h, qs) in rt[r]:
                if h != core:
                    continue
                got = [len(e) for (d, _, e) in first_hop(r) if d == core][0]
                engs = topo.engines(core, cores[qs[0]])
                for t in range(NR):
                    g.wait_ge(sem["arr%d" % t], got)
                    ids = []
                    for q in qs:
                        rid, pid = topo.addr(cores[q], core)
                        ids.append(DstId(rid=rid, pnc=pid))
                    tr = RemoteDMATransfer(dst_ids=ids, dma_engine_mask=bits(engs), remote_sem=sem["arr%d" % t],
                                           src=T["land%d" % t][:, 0:256], dsts=[slot(t, r, q) for q in qs])
                    g.remote_dma_fused([tr], local_sem=sem["sent"])
                g.wait_ge(sem["sent"], NR * len(engs))
        return

    arrivals = 0
    for r in range(n):
        for (h, qs) in rt[r]:
            if rank in qs:
                arrivals += len(topo.engines(h, cores[qs[0]]))

    Q = {"v": g.vector, "a": g.scalar, "t": g.tensor, "g": g, "s": g.sync}
    SN = {"v": "cv", "a": "ca", "t": "ct", "g": "cg"}
    cnt = {}
    known = {e: {} for e in Q}
    recs = {}
    ndma = [0]
    nodes = []

    def R(name, a=None, b=None, s=1, p=None):
        t = T[name]
        if a is None:
            a, b = 0, t.shape[1]
        ps = slice(0, 128) if p is None else slice(*p)
        two = SCRATCH[name][2] in ("bfloat16", "uint16")
        return (t[ps, a:b:s] if s != 1 else t[ps, a:b], [(name, a, b)], [], len(range(a, b, s)), two)

    def IX(win, off):
        return (win[0].indirect(off[0]), win[1], off[1], 16 * off[3], win[4])

    def need(e, tok):
        if known[e].get(tok[0], 0) < tok[1]:
            Q[e].wait_ge(sem[tok[0]], tok[1])
            known[e][tok[0]] = tok[1]

    gate = []

    def emit(e, fn, outs, ins, kind="c", rate=1.0, time=None, cycles=0, late=0.0):
        wr, rd = [], []
        full = [x for x in ins if isinstance(x, tuple)]
        for o in outs:
            wr += o[1]
            rd += o[2]
        for i in full:
            rd += i[1] + i[2]
        if time is not None:
            cost = (time, cycles, 0, 0)
        elif outs[0][2]:
            cost = (T_INDIRECT, 0, 0, outs[0][3])
        elif any(i[2] for i in full):
            cost = (T_INDIRECT, 0, outs[0][3], 0)
        else:
            if rate == 0.5 and not (outs[0][4] and all(i[4] for i in full if i[3] > 1)):
                rate = 1.0
            cost = (T_CALL, max(64.0, rate * max([outs[0][3]] + [i[3] for i in full])), 0, 0)
        time = cost[0] + PACES[0][0] * (cost[1] + PACES[0][1] * cost[2] + PACES[0][2] * cost[3])
        who = e if kind == "c" else "x%d" % len(nodes)
        deps = set(gate)
        for w, regs in ((True, wr), (False, rd)):
            for (nm, a, b) in regs:
                ps = SCRATCH[nm][0] == "psum"
                for (a2, b2, nd, w2, e2) in recs.get(nm, []):
                    if (ps and (e2 != e or e == "t")) or (a < b2 and a2 < b and (w or w2)):
                        deps.add(nd)
        me = len(nodes)
        nodes.append({"e": e, "fn": fn, "kind": kind, "time": time, "cost": cost, "late": late, "deps": deps})
        for (nm, a, b) in wr:
            ps = SCRATCH[nm][0] == "psum"
            recs[nm] = [x for x in recs.get(nm, []) if not (a <= x[0] and x[1] <= b) and not (ps and e == "t")]
            recs[nm].append((a, b, me, True, who))
        for (nm, a, b) in rd:
            recs.setdefault(nm, []).append((a, b, me, False, who))
        return me

    def issue():
        m = len(nodes)
        kids = [[] for _ in range(m)]
        for i, nd in enumerate(nodes):
            for d in nd["deps"]:
                kids[d].append(i)
        rest = [0.0] * m
        for i in range(m - 1, -1, -1):
            rest[i] = nodes[i]["time"] + nodes[i]["late"] + max([rest[k] + T_WAKE for k in kids[i]] + [0.0])
        pars = [sorted(nd["deps"]) for nd in nodes]
        eng = ["h" if "head" in nd else nd["e"] for nd in nodes]
        names = list(Q) + ["h"]

        def plan(before, after, prio, back):
            left = [len(x) for x in before]
            at = [nodes[i]["late"] if back else 0.0 for i in range(m)]
            ready = {e: [i for i in range(m) if left[i] == 0 and eng[i] == e] for e in names}
            free = {e: 0.0 for e in names}
            end = [0.0] * m
            seq = []
            for _ in range(m):
                t1, e = min((min(max(at[i], free[e]) + nodes[i]["time"] for i in ready[e]), e) for e in names if ready[e])
                t0 = max(min(at[i] for i in ready[e]), free[e])
                i = max([j for j in ready[e] if at[j] <= t0 + T_LOOK * (t1 - t0)], key=lambda j: (prio[j], -j))
                ready[e].remove(i)
                seq.append(i)
                free[e] = max(at[i], free[e]) + nodes[i]["time"]
                end[i] = free[e] + (0.0 if back else nodes[i]["late"])
                for k in after[i]:
                    at[k] = max(at[k], end[i] + T_WAKE + (nodes[k]["late"] if back else 0.0))
                    left[k] -= 1
                    if left[k] == 0:
                        ready[eng[k]].append(k)
            return max(end), end, seq

        paces = [([nd["cost"][0] + c * (nd["cost"][1] * (pe if nd["e"] == "t" else 1.0) + ga * nd["cost"][2] + sc * nd["cost"][3]) for nd in nodes],
                  [nd["late"] * (ex if nd["kind"][:3] == "arr" else dm) for nd in nodes], wk) for (c, ga, sc, wk, ex, pe, dm) in PACES]

        waits = [[d for d in pars[i] if not (eng[d] == "t" and eng[i] == "t")] for i in range(m)]

        def replay(seq, pace, old=None, a=0):
            time, late, wake = pace
            free = {e: (0.0, -1) for e in names}
            if old is None:
                end, start, why = [0.0] * m, [0.0] * m, [-1] * m
            else:
                start, why, end = list(old[1]), list(old[2]), list(old[3])
                for i in seq[:a]:
                    free[eng[i]] = (start[i] + time[i], i)
            for i in seq[a:]:
                t0, w = free[eng[i]]
                for d in waits[i]:
                    if end[d] + wake > t0:
                        t0, w = end[d] + wake, d
                start[i], why[i] = t0, w
                free[eng[i]] = (t0 + time[i], i)
                end[i] = t0 + time[i] + late[i]
            return max(end), start, why, end

        def score(seq):
            return sum(replay(seq, p)[0] / w for p, w in zip(paces, norm))

        def rescore(new, a, runs):
            runs = [replay(new, p, r, a) for p, r in zip(paces, runs)]
            return sum(r[0] / w for r, w in zip(runs, norm)), runs

        if m not in ORDER:
            best = None
            prio = rest
            rnd = [SEED]

            def draw():
                rnd[0] = (rnd[0] * 1103515245 + 12345) % 2147483648
                return rnd[0] / 2147483648

            for _ in range(PASSES):
                span, end, seq = plan(pars, kids, prio, False)
                if best is None:
                    norm = [replay(seq, p)[0] for p in paces]
                val = score(seq)
                if best is None or val < best[0]:
                    best = (val, seq, end, span)
                end = list(best[2] if span > best[3] + 1.0 else end)
                for i in range(m):
                    end[i] += SHAKE * draw()
                prio = plan(kids, pars, end, True)[1]
            val, seq = best[0], best[1]
            kept = (val, seq)
            runs = [replay(seq, p) for p in paces]
            for step in range(SWAPS):
                if val < kept[0]:
                    kept = (val, seq)
                slack = 1e-9 + HEAT * (1 - step / SWAPS) ** 2 * draw() * draw()
                span, start, why, end = runs[int(draw() * len(paces))]
                seq = sorted(seq, key=lambda i: start[i])
                chain = []
                i = end.index(span)
                while why[i] >= 0:
                    if why[i] not in nodes[i]["deps"]:
                        chain.append((why[i], i))
                    i = why[i]
                if not chain:
                    continue
                j, i = chain[int(draw() * len(chain))]
                if draw() < 0.35:
                    mine = [k for k in seq[:seq.index(i)] if eng[k] == eng[i]]
                    j = mine[max(0, len(mine) - 1 - int(draw() * draw() * 10))]
                    b = seq.index(j)
                    a = b
                    while a > 0 and seq[a - 1] not in nodes[j]["deps"]:
                        a -= 1
                    if a == b:
                        continue
                    a += int(draw() * (b - a))
                    new = seq[:a] + [j] + seq[a:b] + seq[b + 1:]
                    v, tried = rescore(new, a, runs)
                    if v <= val + slack:
                        val, seq, runs = v, new, tried
                    continue
                a, b = seq.index(j), seq.index(i)
                early, rest_, moved = [], [], {j}
                for k in seq[a + 1:b + 1]:
                    if moved & nodes[k]["deps"]:
                        moved.add(k)
                        rest_.append(k)
                    else:
                        early.append(k)
                if i in moved:
                    continue
                tail = []
                for k in seq[b + 1:b + 1 + int(draw() * draw() * 40)]:
                    if moved & nodes[k]["deps"]:
                        break
                    tail.append(k)
                new = seq[:a] + early + tail + [j] + rest_ + seq[b + 1 + len(tail):]
                v, tried = rescore(new, a, runs)
                if v <= val + slack:
                    val, seq, runs = v, new, tried
            val, seq = min(kept, (val, seq))
            ORDER[m] = (val, seq, [replay(seq, p)[0] for p in paces])
        tok = [None] * m
        head = [i for i in range(m) if "head" in nodes[i]]
        for i in head + [i for i in ORDER[m][1] if i not in head]:
            nd = nodes[i]
            e = nd["e"]
            toks = {}
            for d in nd["deps"]:
                if not (e == "t" and nodes[d]["e"] == "t"):
                    toks[tok[d][0]] = max(toks.get(tok[d][0], 0), tok[d][1])
            for k in sorted(toks):
                need(e, (k, toks[k]))
            ins_ = nd["fn"]()
            if nd["kind"] == "dma":
                s_ = "d%d" % ndma[0]
                ndma[0] += 1
                ins_.then_inc(sem[s_], 16)
                cnt[s_] = 16
            elif nd["kind"] == "c":
                s_ = SN[e]
                ins_.then_inc(sem[s_], 1)
                cnt[s_] = cnt.get(s_, 0) + 1
            else:
                s_ = nd["kind"]
                cnt[s_] = arrivals
            tok[i] = (s_, cnt[s_])
        for k in sorted(cnt):
            need("g", (k, cnt[k]))

    def A_(x):
        return x[0] if isinstance(x, tuple) else x

    def cp(out, in_):
        emit("v", lambda: g.vector.tensor_copy(out[0], in_[0]), [out], [in_], rate=0.5)

    def tt(out, a, b, op):
        ps = any(SCRATCH[x[1][0][0]][0] == "psum" for x in (a, b))
        emit("v", lambda: g.vector.tensor_tensor(out[0], a[0], b[0], op), [out], [a, b], rate=1.0 if ps else 2.0)

    def ts(out, a, s1, op0, s2=None, op1=None):
        if op1 is None:
            emit("v", lambda: g.vector.tensor_scalar(out[0], a[0], A_(s1), None, op0), [out], [a, s1], rate=0.5)
        else:
            emit("v", lambda: g.vector.tensor_scalar(out[0], a[0], A_(s1), A_(s2), op0, op1), [out], [a, s1, s2], rate=0.5)

    def scan(out, d0, d1, init, op0, op1):
        emit("v", lambda: g.vector.tensor_tensor_scan(out[0], d0[0], d1[0], init, op0, op1), [out], [d0, d1], rate=0.5)

    def act(out, in_, f, bias=0.0, scale=1.0, acc=None):
        if out[2]:
            emit("a", lambda: g.scalar.activation(out[0], in_[0], f), [out], [in_])
        elif acc is None:
            emit("a", lambda: g.scalar.activation(out[0], in_[0], f, bias=A_(bias), scale=A_(scale)), [out], [in_, bias, scale])
        else:
            emit("a", lambda: g.scalar.activation(out[0], in_[0], f, bias=A_(bias), scale=A_(scale), accum_out=acc[0]), [out, acc], [in_, bias, scale])

    def aff(out, in_, scale=1.0, bias=0.0):
        act(out, in_, AF.Identity, bias=bias, scale=scale)

    def onehot(out, tmp, in_, neg):
        act(tmp, in_, AF.Abs, bias=neg)
        act(out, tmp, AF.Relu, bias=1.0, scale=-1.0)

    def mm(items, first=True, last=True, wide=1):
        def fn():
            r_ = None
            for i, (o, l, r) in enumerate(items):
                r_ = g.tensor.matmul(o[0], l[0], r[0], first and i == 0, last and i == len(items) - 1)
            return r_
        emit("t", fn, [x[0] for x in items], [x[1] for x in items] + [x[2] for x in items],
             time=0.0, cycles=sum(max(64, x[2][3]) * T_PE * wide + C_PE for x in items))

    def iota(out, pat, base=0, cm=0):
        emit("g", lambda: g.iota(out[0], pat, base, cm, allow_small_or_imprecise_dtypes=True), [out], [],
             time=0.15, cycles=2 * out[3])

    def select(x, pat, op, c, base, cm):
        emit("g", lambda: g.affine_select(x[0], x[0], pat, op, c, base, cm), [x], [x], time=0.2, cycles=2 * x[3])

    def memset(out, c):
        emit("v", lambda: g.vector.memset(out[0], c), [out], [], rate=0.5)

    def fill(out, c):
        iota(out, [[0, out[3]]], c)

    landed = [T_DMA]

    def load(e, out, src, rows, size):
        landed[0] += rows * (T_ROW + size * T_BYTE)
        nodes[emit(e, lambda: Q[e].dma_start(out[0], src), [out], [], kind="dma", time=0.0, late=landed[0])]["head"] = True

    def store(e, dst, in_, rows, size):
        emit(e, lambda: Q[e].dma_start(dst, in_[0]), [], [in_], kind="dma", time=0.1, late=T_DMA + rows * (T_ROW + size * T_BYTE))

    def move(out, in_):
        emit("s", lambda: g.sync.dma_start(out[0], in_[0]), [out], [in_], kind="dma", time=0.1, late=T_DMA + 0.5)

    def slots(buf, w):
        names = {}

        def f(name, a=0, b=None, s=1, k=1, p=None):
            if name not in names:
                names[name] = (sum(x[1] for x in names.values()), k)
            o, kk = names[name]
            return R(buf, o * w + a, o * w + (kk * w if b is None else b), s, p)
        return f

    Bt, Ft, Jt, Mt = slots("B", 256), slots("F", 272), slots("J", 272), slots("M", 144)
    sf, si, su, cf = slots("sf", 16), slots("si", 16), slots("su", 16), slots("cf", 1)

    def P(i, a, b):
        return R("p%d" % i, a, b)

    def to_list(out, z, src):
        nm, a, b = src[1][0]
        mm([(out, Mt(z, 15 - y, 143 - y), R(nm, a + y, b, 16)) for y in range(16)])

    def col(name, i):
        return cf(name, i, i + 1)

    def sq(name):
        return Mt(name, 0, 128)

    LP = R("PT", 2048, 2304)

    def quarter(name, i):
        return (T[name][32 * i:32 * i + 32, :], [(name, 200 + i, 201 + i)], [], 128, name == "EA")

    def whole(name):
        return (T[name][:, :], [(name, 0, 204)], [], 128, name == "EA")

    for i, src in enumerate((T.e0, T.e0, T.h0, T.h0)):
        load("sa"[i // 2], quarter("EH", i), src[:], 2, 512)
    load("s", Jt("wn", 0, 128), T.w0[:], 8, 512)
    load("a", R("VE", 0, 512), T.v0[:], 8, 1024)
    for h in range(2):
        load("s", R("XE", 1024 * h, 1024 * h + 1024), T.x0[:, 1024 * h:1024 * h + 1024], 8, 2048)
    load("s", R("XE", 2048, 2304), T.v0[:, 0:256], 8, 512)
    load("s", R("thb", 0, 3), T.th[:], 8, 6)

    iota(si("p", 0, 1), [[0, 1]], 0, 1)
    iota(sf("c1"), [[1, 16]])
    iota(Ft("n", 0, 144), [[1, 144]])
    iota(sf("l1"), [[16, 8], [0, 2]])
    iota(Bt("num"), [[1, 256]])
    iota(R("ZS"), [[1, 4], [4, 8], [32, 16]], 0, -1)
    iota(Ft("k", 0, 256), [[1, 16], [0, 16]])
    iota(sf("c16"), [[16, 16]])
    iota(Ft("j17", 0, 17), [[16, 17]])
    iota(Ft("pr"), [[-4096, 272]], 272 * 4096)
    fill(Jt("v", 256, 272), 2048)
    fill(R("VE", 512, 1536), 0)

    def late_fills():
        iota(sf("d4", k=2), [[-256, 2], [16, 16]], 512)
        fill(R("S2", 0, 1792), 64)
        fill(R("S2", 1792, 1808), 0)
        fill(Ft("two", 0, 256), 128)
        fill(R("CE", 0, 8), 0)
        fill(sf("D4", 32, 48, k=4), 512)

    ts(si("p", 1, 2), si("p", 0, 1), 15, AL.bitwise_and)
    ts(si("p", 2, 3), si("p", 0, 1), 4, AL.arith_shift_right)
    ts(si("p", 3, 4), si("p", 0, 1), 7, AL.bitwise_and)
    ts(si("p", 4, 5), si("p", 0, 1), 4, AL.arith_shift_right, 1, AL.bitwise_and)
    ts(si("p", 5, 6), si("p", 0, 1), 3, AL.arith_shift_right, 1, AL.bitwise_and)
    ts(si("p", 6, 7), si("p", 0, 1), 1, AL.arith_shift_right, 7, AL.bitwise_and)
    cp(cf("b", 0, 7, k=8), si("p", 0, 7))
    pf, pm, gi, p7, g0, h8, pq = [col("b", i) for i in range(7)]
    ts(cf("t0"), g0, 16.0, AL.mult, h8, AL.add)
    ts(cf("t1"), p7, 32.0, AL.mult, cf("t0"), AL.add)
    ts(su("L1"), sf("l1"), pm, AL.add)
    ts(R("ZS"), R("ZS"), 0.0, AL.is_equal)
    ts(su("L2", 0, 8), sf("c1", 0, 8), 2.0, AL.mult, cf("t1"), AL.add)
    ts(cf("wm"), pm, 2.0, AL.mult, 1.0, AL.add)
    ts(cf("zt"), gi, 16.0, AL.mult, 15.0, AL.add)
    ts(su("Lb"), sf("c1"), 0.0, AL.mult, pm, AL.add)
    ts(Mt("mark"), Ft("n", 0, 144), cf("zt"), AL.is_equal, cf("wm"), AL.mult)

    aff(cf("nb", 0, 7, k=8), cf("b", 0, 7), -1.0)
    onehot(cf("oh", k=16), sf("tmp"), sf("c1"), col("nb", 1))
    aff(cf("t4"), col("oh", 3), 4.0, col("oh", 8))
    aff(cf("bias0"), col("oh", 1), 4.0, cf("t4"))
    onehot(Mt("eye"), Ft("tmp", 0, 144), Ft("n", 0, 144), col("nb", 0))
    aff(cf("pass"), col("oh", 6), -1.0, 1.0)
    aff(cf("rb"), col("oh", 6), -5.0)
    aff(Mt("d5"), Mt("eye"), col("oh", 5))
    aff(cf("bias1"), col("oh", 4), 256.0, cf("bias0"))
    aff(Mt("dg"), Mt("eye"), cf("pass"))
    onehot(cf("q", k=8), sf("tmp", 0, 8), sf("c1", 0, 8), col("nb", 6))
    act(Mt("one"), Mt("mark"), AF.Sign)
    aff(cf("t5"), col("q", 3), -16777216.0)
    aff(cf("t6"), col("q", 1), 4.0, cf("t5"))
    aff(cf("wk"), col("q", 0), 16384.0, cf("t6"))
    aff(Mt("key"), Mt("one"), cf("wk"))
    aff(Mt("id"), Mt("one"), col("q", 2))
    aff(Mt("neye"), Mt("eye"), -1.0)
    act(Ft("k2", 0, 256), Ft("k", 0, 256), AF.Square, bias=0.5)
    aff(Ft("kap", 0, 256), Ft("k2", 0, 256), 1.0, 0.75)
    aff(sf("lane"), sf("c16"), 1.0, pm)

    def tile(t):
        cp(si("m"), P(2, 0, 16))
        ts(si("u"), si("m"), 4095, AL.bitwise_and)
        tt(si("sq"), si("u"), si("u"), AL.mult)
        tt(Ft("t1", 0, 256), IX(si("u"), su("Lb")), Ft("kap", 0, 256), AL.mult)
        ts(si("sh"), si("sq"), 5, AL.arith_shift_right)
        if t > 0:
            ts(sf("base"), si("sh"), cf("A"), AL.add)
        tt(Jt("s", 0, 256), IX(sf("base") if t > 0 else si("sh"), su("Lb")), Ft("t1", 0, 256), AL.add)
        ts(Jt("a", 0, 256), Jt("s", 0, 256), 2047, AL.bitwise_and)
        cp(su("tile", k=16), Jt("a", 0, 256))

    def codes():
        tt(Ft("code"), IX(Jt("a"), su("Lp", 0, 17, k=2)), Ft("pr"), AL.add)

    cp(whole("EA"), whole("EH"))
    for i in (1, 3):
        tt(quarter("EA", i), quarter("EH", i), quarter("EA", i), AL.subtract)
    to_list(P(2, 0, 16), "mark", R("VE", 0, 256))
    for h in range(2):
        mm([(P(4 + h, 0, 256), sq("d5"), Bt("num"))], last=False)
        mm([(P(4 + h, 128 * j, 128 * j + 128), R("ZS", 256 * h + 128 * j, 256 * h + 128 * j + 128), whole("EA")) for j in range(2)], first=False)
        act(R("SP", 256 * h, 256 * h + 256), P(4 + h, 0, 256), AF.Identity, bias=cf("bias%d" % h))
    cp(Ft("w2", 0, 256), IX(Jt("wn", 0, 128), su("L1")))
    emit("v", lambda: g.vector.transpose(Ft("w3", 0, 256)[0], Ft("w2", 0, 256)[0]), [Ft("w3", 0, 256)], [Ft("w2", 0, 256)])
    cp(su("Wl", k=8), IX(Ft("w3", 0, 256), su("L2", 0, 8)))
    for c in range(2):
        act(R("PT", 1024 * c, 1024 * c + 1024), IX(R("SP", 0, 512), su("Wl", 64 * c, 64 * c + 64)), AF.Copy)
    act(LP, R("SP", 0, 256), AF.Copy)

    def blk(c):
        return 512 * c, 512 * c + 512, su("Wl", 32 * c, 32 * c + 32)

    def greater_v(c, nv):
        a, b, l = blk(c)
        tt(R("GT", a, b), IX(R("VE", 0, nv), l), R("XE", a, b), AL.is_le)

    def fetch_a(c, nv):
        a, b, l = blk(c)
        act(R("VW", a, b), IX(R("VE", 0, nv), l), AF.Copy)
        mm([(P(6 + c % 2, 0, 512), sq("neye"), R("VW", a, b)), (P(6 + c % 2, 0, 512), sq("eye"), R("XE", a, b))])

    def greater_a(c):
        a, b, l = blk(c)
        act(R("GT", a, b), P(6 + c % 2, 0, 512), AF.Sign, bias=0.5)

    def count(c, signs):
        a, b, l = blk(c)
        mm([(P(4 + c % 2, 0, 512), sq("dg"), R("PT", a, b)), (P(4 + c % 2, 0, 512), Mt("one", 9, 137), R("GT", a, b))])
        act(R("PT", a, b), P(4 + c % 2, 0, 512), AF.Relu, bias=cf("rb2" if signs else "rb"))

    def lane_keys():
        to_list(P(3, 0, 16), "key", LP)
        aff(sf("cd"), P(3, 0, 16), 1.0, -float(4096 * 2048 + 2048))
        act(Ft("cb", 0, 256), IX(sf("cd"), su("Lb")), AF.Copy)

    for c in range(4):
        greater_v(c, 512)
        count(c, False)
    tile(0)
    lane_keys()

    def cur(t):
        return sf("cur", 16 * t, 16 * t + 16, k=3)

    def sp(t):
        return sf("sp", PLACE[t], PLACE[t] + 16, k=4)

    def pre(t):
        tt(sf("cdm"), cur(t), sf("dum"), AL.subtract)
        aff(sf("dn"), sf("cdm"), -1.0, float(512 + 256 * t - 1280))
        aff(sf("T4", PLACE[t], PLACE[t] + 16, k=4), sf("cdm"), 1.0, float(768 + 1280 - 512 + 256 * t))
        if t > 0:
            aff(sf("c2"), cur(t), 1.0, 1.0)

    def spawn_block(t):
        o = P(5, 0, 256)
        mm(([(o, sq("dg4"), LP)] if t < 2 else []) + [(o, sq("d5"), Bt("num"))])
        act(R("SP", 512 + 256 * t, 768 + 256 * t), o, AF.Identity, bias=col("bs", t) if t < 2 else col("b4", t))

    def constants_1():
        aff(Ft("j17", 17, 34), Ft("j17", 0, 17), 1.0, pm)
        aff(Ft("j17", 34, 51), Ft("j17", 17, 34), -16.0, 256.0)
        aff(sf("dum"), sf("lane"), 1.0, 1280.0)
        aff(cur(0), sf("lane"))
        ts(Jt("x17", 0, 17), Ft("j17", 17, 34), 8.0, AL.subtract, 1.0 / 17, AL.mult)
        ts(Jt("a", 256, 272), sf("lane"), 2048.0, AL.add)
        ts(Ft("j17", 51, 68), Jt("x17", 0, 17), 273.0, AL.mult)
        tt(Ft("j17", 68, 85), Ft("j17", 34, 51), Ft("j17", 51, 68), AL.add)
        cp(su("Lp", 0, 17, k=2), Ft("j17", 68, 85))

    def constants_2():
        aff(cf("nth", k=3), R("thb", 0, 3), -1.0, 0.5)
        aff(cf("t7"), col("q", 1), 1.0, col("oh", 8))
        aff(cf("p4"), col("q", 0), 1.0, cf("t7"))
        aff(cf("dl"), col("oh", 3), -1.0, col("oh", 1))
        aff(Mt("dg4"), Mt("eye"), cf("p4"))
        aff(cf("b3", k=3), sf("c1", 0, 3), 256.0, 512.0)
        aff(cf("b4", k=3), cf("b3"), col("oh", 4))
        for t in range(2):
            aff(cf("bs", t, t + 1, k=2), cf("dl"), 0.5 ** (t + 1), col("b4", t))
        fill(sq("bd"), 1)
        select(sq("bd"), [[-16, 8], [0, 16]], AL.is_ge, 0.0, 0, 1)
        select(sq("bd"), [[16, 8], [0, 16]], AL.is_ge, 0.0, 15, -1)
        aff(sf("l16"), sf("lane"), 1.0 / 16)
        aff(sf("l8"), sf("lane"), 8.0)
        aff(cf("rb2"), col("oh", 6), 5.0)

    def constants_3():
        memset(sf("hf"), 0.5)
        scan(sf("pw"), sf("hf"), sf("hf"), 1.0, AL.mult, AL.mult)
        tt(sf("hf"), sf("pw"), cf("oh"), AL.mult)
        act(sf("pw"), sf("hf"), AF.Identity, acc=cf("w4"))
        aff(sq("bdw"), sq("bd"), cf("w4"))
        aff(cf("thr"), cf("w4"), 2.0)
        aff(cf("wi1"), col("q", 2), 1.0, col("oh", 8))
        aff(sq("bdid"), sq("bd"), cf("wi1"))
        gate.append(made)
        fill(Mt("row", 0, 128, p=(0, 16)), 1)
        select(Mt("row", 0, 128, p=(0, 16)), [[0, 8], [1, 16]], AL.is_equal, 0.0, 0, -1)
        fill(Bt("nm", p=(0, 16)), 65536)
        select(Bt("nm", p=(0, 16)), [[0, 16], [1, 16]], AL.not_equal, 0.0, 0, -1)
        fill(Bt("rst"), 0)
        select(Bt("rst"), [[0, 16], [1, 16]], AL.is_gt, 2097152.0, 0, 0)
        gate.pop()

    def constants_4():
        aff(cf("m4"), col("oh", 8), -4.0)
        aff(cf("weh", k=2), cf("q", 0, 2), 1.0, cf("m4"))
        for i, nm in enumerate(("e", "h")):
            aff(Mt(nm), Mt("one"), col("weh", i))
            to_list(P(1, 32 * i, 32 * i + 32), nm, R("SP", 0, 512))
        cp(su("eh", k=4), P(1, 0, 64))

    def inverse(i):
        if i == 0:
            iota(R("RA"), [[1, 512]], 64)
            aff(R("Z0"), Mt("one"), col("oh", 0))
        for h in range(2):
            act(IX(R("WF", 768, 1280), su("eh", 32 * i + 16 * h, 32 * i + 16 * h + 16)), R("RA", 256 * h, 256 * h + 256), AF.Silu)
            if i + h == 0:
                nd = nodes[-1]
                nd["cost"] = (nd["cost"][0], 1570, 0, nd["cost"][3])
                nd["time"] += 1.5
        for h in range(4):
            mm([(P(1, 0, 32), R("Z0", 15 - y, 143 - y), R("WF", 768 + y, 1280, 16)) for y in range(4 * h, 4 * h + 4)],
               first=(h == 0), last=(h == 3), wide=4)
        ts(su("inv", 32 * i, 32 * i + 32, k=4), P(1, 0, 32), 64.0, AL.subtract)

    def constants_6():
        aff(cf("sg"), col("oh", 1), -1.0, col("oh", 0))
        aff(cf("sg64"), cf("sg"), 1.0 / 64)
        aff(cf("oh64", k=2), cf("oh", 0, 2), 1.0 / 64)
        aff(sf("D4", 0, 32), sf("d4"), 1.0, pm)
        aff(sf("D4", 48, 64), sf("lane"))
        aff(sf("T4", 32, 48), sf("lane"), 1.0, -512.0)
        aff(sp(3), sp(0))
        aff(sf("l8b", 0, CUT), sf("l8", 0, CUT))
        aff(sf("l8b", CUT, 16), sf("l8", CUT, 16), 1.0, -128.0 * CUT)

    def constants_5():
        gate.append(made)
        fill(R("MK"), 1)
        fill(R("RR", 0, 768), 0)
        fill(R("WF", 0, 768), -2)
        gate.pop()
        move(R("RR", 0, 768, p=(0, 128, 16)), R("WF", 0, 768, p=(0, 8)))

    constants_1()

    for t in range(NR):
        land = "land%d" % t
        for c in range(4):
            k0, k1 = 4 * c, 4 * c + 4
            if c == 0 and NP[t]:
                cp(R("G", 0, 256 * NP[t]), IX(R("PT", 0, 2048), su("tile", 0, 16 * NP[t])))
                k0 = NP[t]
            if k0 < k1:
                act(R("G", 256 * k0, 256 * k1), IX(R("PT", 0, 2048), su("tile", 16 * k0, 16 * k1)), AF.Copy)
        for c in ([1, 0, 2, 3] if NP[t] else range(4)):
            to_list(P(1 if c == 3 else 0, 64 * c, 64 * c + 64), "key", R("G", 1024 * c, 1024 * c + 1024))
        na = NA[t]
        n2 = 16 - na
        np_ = na + 2

        def cand(k):
            return IX(R("XE", 0, 2048), su("tile", 16 * k, 16 * k + 16))

        def piece(j):
            return (T.PC[:, j:256 * np_:np_], [("PC", 256 * j, 256 * j + 256)], [], 256, True)

        for k in range(n2):
            o = piece(k - n2 + 2) if k >= n2 - 2 else Bt("mx%d" % (k % 4))
            if k < 2:
                cp(o, cand(k))
            else:
                tt(o, cand(k), Bt("mx%d" % ((k - 2) % 4)), AL.max)
        for j in range(na):
            act(piece(2 + j), cand(n2 + j), AF.Copy)
        if t == 0 or na != NA[t - 1]:
            iota(R("RS", 0, 256 * np_), [[0, 256], [256, np_]])
            aff(sf("top"), sf("lane"), float(np_), float(1536 + np_ - 1))
        scan(R("VE", 1536, 1536 + 256 * np_), R("RS", 0, 256 * np_), R("PC", 0, 256 * np_), 0.0, AL.min, AL.max)
        if t == 0:
            codes()
        if t == 1:
            to_list(P(6, 0, 128), "id", R("PT", 0, 2048))
        tt(Jt("v", 0, 192), P(0, 0, 192), Ft("cb", 0, 192), AL.subtract)
        tt(Jt("v", 192, 256), P(1, 192, 256), Ft("cb", 192, 256), AL.subtract)
        ts(Jt("tb"), IX(Jt("v"), su("Lp", 0, 17)), 11, AL.arith_shift_right, 0x1001 | (1 << 20), AL.bitwise_and)
        ts(Jt("nn"), Jt("tb"), 1.0 / 4096, AL.mult, 0.5 - 1.0 / 8192, AL.add)
        ts(Ft("nh"), Jt("nn"), 1.0, AL.not_equal)
        scan(Ft("sc"), Ft("nh"), Ft("code"), 0.0, AL.mult, AL.max)
        cp(si("s"), Ft("sc", 16, 272, 17))
        ts(si("al"), si("s"), 4095, AL.bitwise_and)
        cp(su("al"), si("al"))
        act(Bt("gf"), IX(R("PT"), su("al")), AF.Copy)
        to_list(P(1, 0, 16), "id", Bt("gf"))
        act(Bt("xf"), IX(R("XE"), su("al")), AF.Copy)
        ts(Bt("nr", 0, 16), si("al"), 2048.0, AL.is_ge)
        tt(sf("tq"), Bt("nr", 0, 16), sf("top"), AL.mult)
        tt(sf("sl"), P(1, 0, 16), sf("tq"), AL.max)
        cp(su("sl"), sf("sl"))
        tt(Bt("df"), IX(R("VE", 0, 1536 + 256 * np_), su("sl")), Bt("xf"), AL.subtract)

        def same_strand(xs):
            for x in xs:
                a = 256 * x
                ts(R("EQ", a, a + 256 - 16 * x), su("curR", 16 * x, 256, k=16), sf("key", x, x + 1), AL.is_equal)
                mm([(P(0, 16 * x, 16 * x + 16), sq("bdw"), R("EQ", a, a + 16))]
                   + ([(P(0, 16 * x + 16, 256), sq("bd"), R("EQ", a + 16, a + 256 - 16 * x))] if x < 15 else []), first=False, last=(x == 15))

        if t > 0:
            tt(sf("key"), Bt("nr", 0, 16), sf("c2"), AL.mult)
            ts(sf("nrt"), si("al"), 2048.0, AL.is_ge, cf("thr"), AL.mult)
            mm([(P(0, 0, 256), Mt("row", 0, 128, p=(0, 16)), Bt("nm", p=(0, 16)))], last=False)
            same_strand(range(0, 2))
        if t == 1:
            cp(su("Wl"), P(6, 0, 128))
        yn = R(land, 0, 256)
        act(yn, Bt("df"), AF.Abs)
        trs = []
        for (d, sl_, engs) in first_hop(rank):
            rid, pid = topo.addr(d, core)
            trs.append(RemoteDMATransfer(dst_ids=[DstId(rid=rid, pnc=pid)], dma_engine_mask=bits(engs), remote_sem=sem["arr%d" % t],
                                         src=yn[0], dst=T[land][:, 256 * sl_:256 * sl_ + 256]))
            cnt["sent"] = cnt.get("sent", 0) + len(engs)
        emit("g", lambda trs=trs: g.remote_dma_fused(trs, local_sem=sem["sent"]), [R(land, 256, 2048)], [yn],
             kind="arr%d" % t, time=0.5, late=T_EXCH[t])
        made = len(nodes) - 2
        if t == 0:
            gate.append(made)
            late_fills()
            gate.pop()
            pre(0)
            constants_2()
            spawn_block(0)
        act(Bt("gs"), yn, AF.Sign, bias=col("nth", t))
        if t > 0:
            same_strand(range(2, 16))
        to_list(P(3, 0, 16), "one", Bt("gs"))
        to_list(P(2, 0, 16), "mark", yn)
        if t > 0:
            scan(Ft("sc", 0, 256), Bt("rst"), P(0, 0, 256), 0.0, AL.add, AL.min)
            tt(sf("lead"), Ft("sc", 15, 256, 16), sf("nrt"), AL.is_lt)
            lead = sf("lead")
        else:
            lead = Bt("nr", 0, 16)
        tt(sf("u3"), sf("cdm"), lead, AL.mult)
        ts(sf("wl"), P(3, 0, 16), 2.0, AL.is_ge)
        tt(sf("u4"), sf("u3"), sf("dum"), AL.add)
        tt(sp(t), sf("wl"), lead, AL.mult)
        tt(sf("a1"), sp(t), sf("dn"), AL.mult)
        nxt = cur(t + 1) if t < 2 else sf("last")
        tt(sf("vo"), sf("u4"), sf("a1"), AL.add)
        tt(nxt, P(1, 0, 16), sf("a1"), AL.add)
        cp(su("vo"), sf("vo"))
        cp(su("nc"), nxt)
        cp(IX(R("VE", 0, 1536), su("vo")), yn)
        written = len(nodes) - 1

        def zlist():
            ts(si("d"), si("u"), 0x70, AL.bitwise_and)
            tt(sf("zz"), si("d"), sf("l16"), AL.add)
            ts(su("zl"), sf("zz"), 16.0, AL.mult)

        def cells_of_arrivals(base):
            to_list(P(2, 0, 16), "mark", Bt("z"))
            cp(si("mz"), P(2, 0, 16))
            ts(si("m7"), si("mz"), 7, AL.bitwise_and)
            tt(sf("bo"), si("m7"), sf(base), AL.add)
            cp(su("bo"), sf("bo"))

        if t < 2:
            nv = 768 + 256 * t
            mm([(P(7, 0, 16), sq("bd"), Bt("nr", 0, 16))])
            gate.append(written)
            move(R("XE", 2048, 2304), yn)
            gate.pop()
            act(sf("tmp"), P(7, 0, 16), AF.Identity, scale=-1.0, bias=16.0, acc=cf("A"))
            act(LP, IX(R("SP", 0, nv), su("nc")), AF.Copy)
            for c in range(NDV):
                greater_v(c, nv)
            for c in range(NDV, 4):
                fetch_a(c, nv)
            act(Bt("vc"), IX(R("VE", 0, nv), su("nc")), AF.Copy)
            for c in range(NDV):
                count(c, False)
            for c in range(NDV, 4):
                greater_a(c)
            tile(t + 1)
            zlist()
            codes()
            for c in range(NDV, 4):
                count(c, True)
            if t == 0:
                constants_3()
                constants_4()
                constants_6()
            else:
                constants_5()
            inverse(t)
            mm([(P(0, 0, 256), sq("bdid"), LP)])
            cp(su("curR", k=16), P(0, 0, 256))
            act(Bt("z"), IX(R(land), su("zl")), AF.Copy)
            tt(Bt("g2"), IX(R(land), su("zl")), Bt("vc"), AL.is_ge)
            mm([(P(6, 0, 256), sq("dg"), LP)], last=False)
            mm([(P(6, 0, 256), Mt("one", 9, 137), Bt("g2"))], first=False)
            act(Bt("lpb"), P(6, 0, 256), AF.Relu, bias=cf("rb"))
            pre(t + 1)
            cells_of_arrivals("l8")
            cp(IX(R("PT", 0, 2048), su("bo")), Bt("lpb"))
            cp(IX(R("XE", 0, 2048), su("bo")), Bt("z"))
            lane_keys()
            spawn_block(t + 1)
        else:
            act(LP, IX(R("SP"), su("nc")), AF.Copy)
            store("s", T.yv[:], R("VE", 0, 1280), 8, 2560)
            for (a, b) in ((0, 48), (48, 64)):
                tt(sf("T4", a, b), sf("T4", a, b), sf("sp", a, b), AL.mult)
                tt(sf("T4", a, b), sf("T4", a, b), sf("D4", a, b), AL.add)
                cp(su("l4", a, b, k=4), sf("T4", a, b))
            cp(si("m"), P(2, 0, 16))
            ts(si("u"), si("m"), 4095, AL.bitwise_and)
            zlist()
            l0, l1, z0, l2 = [su("l4", 16 * i, 16 * i + 16) for i in range(4)]
            act(IX(R("S2", 0, 1792), l2), Ft("two", 0, 256), AF.Silu)
            act(Ft("g1", 0, 256), IX(R("S2", 0, 1536), l1), AF.Copy)
            act(Bt("z"), IX(R(land), su("zl")), AF.Copy)
            tt(IX(R("S2", 0, 1536), l1), Ft("g1", 0, 256), R("S2", 1536, 1792), AL.add)
            aff(Bt("q1"), Ft("g1", 0, 256), cf("sg64"))
            act(Bt("q0"), IX(R("S2", 0, 1536), l0), AF.Identity, scale=cf("sg64"))
            act(R("S0", 256, 512), R("S2", 1024, 1280), AF.Copy)
            tt(R("S0", 0, 256), IX(R("S2", 1280, 1808), z0), R("S2", 768, 1024), AL.add)
            act(R("SE", 0, 512), IX(R("S0"), su("inv", 0, 32)), AF.Identity, scale=col("oh64", 0))
            ts(R("SE", 512, 1024), IX(R("S0"), su("inv", 32, 64)), col("oh64", 1), AL.mult)
            cells_of_arrivals("l8b")
            cuts = ((0, CUT), (CUT, 16))
            for (a, b) in cuts:
                cp(IX(R("XE", 128 * a, 128 * b), su("bo", a, b)), Bt("z", 16 * a, 16 * b))
                store("s", T.yx[:, 128 * a:128 * b], R("XE", 128 * a, 128 * b), 8, 6000 if a == 0 else 4400)
                gate[:] = [len(nodes) - 2] if a == 0 else []
            scan(R("CE", 1, 513), R("MK"), R("SE", 0, 512), 0.0, AL.mult, AL.add)
            for h in range(2):
                act(R("RA", 256 * h, 256 * h + 256), IX(R("CE", 0, 513), su("eh", 16 * h, 16 * h + 16)), AF.Identity, bias=col("oh", 0))
            for (a, b) in cuts[::-1]:
                cp(IX(R("PT", 128 * a, 128 * b), su("bo", a, b)), R("PT", 2048 + 16 * a, 2048 + 16 * b))
                mm([(P(6, 0, 128), Mt("id", 15 - y, 143 - y), R("PT", 128 * y, 128 * y + 128)) for y in range(a, b)],
                   first=(a > 0), last=(a == 0))
            act(Ft("wo", 0, 128), P(6, 0, 128), AF.Copy)
            store("a", T.yw[:], Ft("wo", 0, 128), 8, 512)
            scan(R("CE", 528, 1040), R("MK"), R("SE", 512, 1024), -1.0, AL.mult, AL.add)
            for h in range(2):
                tt(R("RR", 768 + 256 * h, 1024 + 256 * h), IX(R("CE", 528, 1040), su("eh", 32 + 16 * h, 48 + 16 * h)),
                   R("RA", 256 * h, 256 * h + 256), AL.add)
            tt(R("RR", 1280, 1536), IX(R("RR", 0, 1280), l0), Bt("q0"), AL.add)
            tt(R("RR", 1536, 1792), IX(R("RR", 0, 1536), l1), Bt("q1"), AL.add)
            act(R("RR", 1792, 2048), IX(R("RR", 0, 1792), l2), AF.Identity, bias=cf("sg"))
            store("s", T.ye[:], R("RR", 768, 2048, p=(0, 128, 16)), 1, 2560)
            store("a", T.yh[:], R("RR", 768, 2048, p=(1, 128, 16)), 1, 2560)

    issue()
